import numpy as np, ml_dtypes
CORES = [36,164,52,180,100,228,116,244]
N = 8
BF = ml_dtypes.bfloat16
def gentries(a):
    return np.ascontiguousarray(a.reshape(8, 16, -1).transpose(0, 2, 1)).reshape(8, -1)
def gtable(e):
    e = np.asarray(e); return np.ascontiguousarray(e.reshape(8, -1, 16).transpose(0, 2, 1)).reshape(128, -1).astype(np.int32)
W, F, C, K, TV, R = 2048, 1024, 256, 3, 4, 8
def num(l, b, t):
    return ((l * b >> 5) + l + 37 * b + 77 * t) & (F - 1)
def parts(rng):
    x = rng.integers(0, 16, (N, 8, 16, W)); fa = rng.integers(0, W, (N, 8, 16, F))
    l = rng.integers(0, W, (N, 8, K, C)); u = np.stack([rng.integers(-1, k, (N, 8, C)) for k in range(K)], axis=2)
    return x, fa, l, u, rng.integers(0, W, (N, 8, C)), rng.integers(36, 76, (N, 8, K)), rng.integers(0, 16, (N, 8, 16))
def pack(x, fa, l, u, e, th, w):
    return {"xs": np.ascontiguousarray(x.reshape(N, 128, W)).astype(np.float32).astype(BF), "fa": np.ascontiguousarray(fa.reshape(N, 128, F)).astype(np.int32),
            "lc": np.stack([gtable(a.reshape(8, -1)) for a in l]), "up": np.stack([gtable(a.reshape(8, -1)) for a in u]), "ex": np.stack([gtable(a) for a in e]),
            "th": np.ascontiguousarray(th).astype(np.int32), "wt": np.ascontiguousarray(w.reshape(N, 128, 1)).astype(np.int32)}
def setup_inputs(rng):
    return pack(*parts(rng))
def setup_inputs_spread(rng):
    x, fa, l, u, e, th, w = parts(rng)
    x = np.minimum((np.exp2(4 * rng.random((N, 8, 1, W))) * rng.random((N, 8, 16, W))).astype(np.int64), 15)
    a = rng.choice(np.array([1, 2, 4]), (N, 8, 1, 1))
    fa = np.minimum((W * rng.random(fa.shape) ** a).astype(np.int64), W - 1); l = np.minimum((W * rng.random(l.shape) ** a).astype(np.int64), W - 1)
    e = np.minimum((W * rng.random(e.shape) ** a[..., 0]).astype(np.int64), W - 1)
    th = np.minimum(np.exp2(8 * rng.random(th.shape)).astype(np.int64) - 1, 255); w = np.minimum(np.exp2(4 * rng.random(w.shape)).astype(np.int64) - 1, 15)
    return pack(x, fa, l, u, e, th, w)
def setup_inputs_ends(rng):
    x, fa, l, u, e, th, w = parts(rng)
    kind = rng.integers(0, 4, (N, 8, 1, W)); x = np.where(kind == 0, 0, np.where(kind == 1, 15, 15 * rng.integers(0, 2, x.shape)))
    x[..., 0] = 0; x[..., W - 1] = 15
    kind = rng.integers(0, 4, (N, 8, 1, F)); end = (W - 1) * rng.integers(0, 2, fa.shape)
    fa = np.where(kind == 0, 0, np.where(kind == 1, W - 1, np.where((kind == 2) | (rng.random(fa.shape) < 0.5), end, fa)))
    l = np.where(rng.random(l.shape) < 0.85, (W - 1) * rng.integers(0, 2, l.shape), l)
    e = np.where(rng.random(e.shape) < 0.85, (W - 1) * rng.integers(0, 2, e.shape), e)
    u = np.where(rng.random(u.shape) < 0.6, -1, np.arange(K)[:, None] - 1)
    th = 255 * rng.integers(0, 2, th.shape); th[:, 0, 0] = 0; th[:, 7] = 255
    w = 15 * rng.integers(0, 2, w.shape); w[:, 0] = 0; w[:, 7] = 15
    e[:, :, C - 1] = W - 1; l[:, :, 0, C - 1] = W - 1; l[:, :, 1, C - 1] = 0; u[:, :, 1, C - 1] = -1; u[:, :, K - 1, 0] = K - 2
    n0, n1 = num(W - 1, W - 1, 0), num(0, W - 1, 0)
    for g in (3, 7):
        x[:, g, :, 1:4] = 0; fa[:, g, :, n0] = rng.integers(0, 4, (N, 16)); fa[:, g, 0, n0] = 3; fa[:, g, 1, n0] = 0; fa[:, g, :, n1] = W - 1
    return pack(x, fa, l, u, e, th, w)
def setup_inputs_corners(rng):
    x, fa, l, u, e, th, w = parts(rng); k = np.arange(K)[:, None]
    for s in range(N):
        for g in range(8):
            m = (g + s) % 8
            if m == 0: u[s, g] = k - 1; th[s, g] = 255; th[s, g, 0] = 0
            if m == 1: u[s, g] = k - 1; th[s, g] = 255
            if m == 2: u[s, g] = -1; th[s, g] = rng.choice(np.array([0, 255]), K); w[s, g] = 0
            if m == 3: u[s, g] = k - 1; th[s, g] = 255; th[s, g, K - 1] = 0; w[s, g] = 15
            if m == 4: u[s, g] = np.minimum(k - 1, 0)
            if m == 5: x[s, g] = rng.integers(0, 16, W); th[s, g] = rng.choice(np.array([0, 1, 16, 17, 32]), K)
            if m == 6: x[s, g] = x[s, g][:, rng.integers(0, 8, W)]
            if m == 7:
                fa[s, g] = fa[s, g, :1].copy(); fa[s, g, :, ::4] = rng.choice(np.array([0, W - 1, W // 2, W // 2 + 1]), (16, F // 4))
                e[s, g] = rng.choice(np.array([0, W - 1, W // 2, 1]), C); l[s, g, ::2] = e[s, g]; th[s, g] = rng.integers(60, 110, K)
    return pack(x, fa, l, u, e, th, w)
def setup_inputs_crowd(rng):
    x, fa, l, u, e, th, w = parts(rng)
    for s in (0, 2):
        for g in range(8):
            x[s, g, :, :8] = 0; o = np.argsort(np.sum(x[s, g], axis=0)); e[s, g] = rng.choice(o[W // 2:], C); one = s == 2 and g == 7
            if one: l[s, g, K - 1, C - 1] = e[s, g, C - 1]; u[s, g, K - 1, C - 1] = -1; th[s, g] = 1
            n = num(l[s, g], e[s, g], 0)
            fa[s, g][:, n.reshape(-1)] = rng.integers(0, 8, (16, K * C))
            if one: fa[s, g, int(rng.integers(0, 16)), n[K - 1, C - 1]] = e[s, g, C - 1]
    for s in range(1, N, 2):
        for g in (0, 4):
            e[s, g] = int(e[s, g, 0]); l[s, g] = l[s, g, :, :1].copy(); u[s, g] = u[s, g, :, :1].copy()
        l[s, 4, :, C - 1] = rng.integers(0, W, K)
    if N > 5: th[5] = 255
    return pack(x, fa, l, u, e, th, w)
def setup_inputs_brink(rng):
    x, fa, l, u, e, th, w = parts(rng); al = np.arange(W); odd = np.arange(1, C, 2)
    pq = np.array([[3, 21], [21, 3], [5, 19], [19, 5], [7, 9], [9, 7]])
    for s in range(N):
        for g in range(8):
            m = (g + s) % 8
            if m < 3: u[s, g] = np.arange(K)[:, None] - 1; th[s, g] = 255
            if m == 0:
                used = np.zeros(F, bool)
                for i in range(C):
                    n = num(al, int(e[s, g, i]), 0); room = np.flatnonzero(~used[n])
                    if len(room) == 0: e[s, g, i] = 0; n = num(al, 0, 0); room = np.flatnonzero(~used[n])
                    v = int(room[int(rng.integers(0, len(room)))]); l[s, g, 0, i] = v; used[n[v]] = True
            if m == 1:
                lo = 512 * int(rng.integers(0, W // 512)); d = int(rng.integers(0, 512)); v = lo + d
                fa[s, g] = lo + rng.integers(0, 512, (16, F)); x[s, g, :, v] = 15
                e[s, g, C - 1] = v; l[s, g, 0, C - 1] = v; n = num(v, v, 0)
                fa[s, g, :15, n] = lo + ((d + rng.integers(1, 512, 15)) & 511); fa[s, g, 15, n] = v
            if m == 2:
                j = pq[rng.integers(0, 6, len(odd))]; l[s, g, 0, odd] = W - j[:, 0]; e[s, g, odd] = W - j[:, 1]
            if m == 3 or m == 4:
                o = rng.permutation(W)[:192]; x[s, g][:, o[:128]] = 0; x[s, g][rng.integers(0, 16, 64), o[64:128]] = 1; x[s, g][:, o[128:]] = 15
                e[s, g, odd] = rng.choice(o[128:], len(odd)); u[s, g][:, odd] = -1
                n = num(l[s, g][:, odd], e[s, g, odd], 0).reshape(-1); c = rng.choice(o[:64], (16, F))
                if m == 4:
                    hit = rng.random((16, F)) < 0.25; hit[0] = False; hit[15] = True
                    c = np.where(hit, rng.choice(o[64:128], (16, F)), c)
                fa[s, g][:, n] = c[:, n]
                th[s, g] = np.resize(np.array([240, 241, 239]) if m == 3 else np.array([240, 239, 241]), K)
    return pack(x, fa, l, u, e, th, w)
def check_inputs(d):
    bad = []
    for k, lo, hi in (("xs", 0, 15), ("fa", 0, W - 1), ("lc", 0, W - 1), ("up", -1, K - 2), ("ex", 0, W - 1), ("th", 0, 255), ("wt", 0, 15)):
        v = np.asarray(d[k]).astype(np.float32)
        if not (np.min(v) >= lo and np.max(v) <= hi): bad.append("range of " + k)
        if k == "xs" and np.any(v != np.floor(v)): bad.append("whole numbers in xs")
    u = np.stack([gentries(a) for a in np.asarray(d["up"])]).reshape(N, 8, K, C)
    if np.any(u > np.arange(K)[:, None] - 1): bad.append("inputs in up that are not rows before")
    return bad
def reference(xs, fa, lc, up, ex, th, wt):
    X = xs.astype(np.float32).astype(np.int32).reshape(N, 8, 16, W); FC = fa.astype(np.int64).reshape(N, 8, 16, F)
    L = np.stack([gentries(a) for a in lc]).astype(np.int64).reshape(N, 8, K, C); U = np.stack([gentries(a) for a in up]).astype(np.int64).reshape(N, 8, K, C)
    E = np.stack([gentries(a) for a in ex]).astype(np.int64); H = th.astype(np.int64); V = wt.astype(np.int64).reshape(N, 8, 16, 1)
    A = np.zeros(N, np.int64)
    for t in range(TV):
        deaths = np.zeros(N, np.int64)
        for s in range(N):
            r = (s - t) % N; l, u, x = L[r], U[r], X[s]
            beta = np.zeros((8, K + 1, C), np.int64); beta[:, 0] = E[s]
            live = np.ones((8, K + 1, C), bool); y = np.zeros((8, 16, C), np.int32)
            for k in range(K):
                j = u[:, k:k + 1] + 1
                b = np.take_along_axis(beta, j, 1)[:, 0]; ok = np.take_along_axis(live, j, 1)[:, 0]
                c = np.take_along_axis(FC[s], num(l[:, k], b, t)[:, None, :], 2)
                q = np.maximum(np.take_along_axis(x, l[:, k:k + 1], 2), np.take_along_axis(x, b[:, None, :], 2))
                v = np.take_along_axis(x, np.ascontiguousarray(c.transpose(0, 2, 1)).reshape(8, 1, 16 * C), 2).reshape(8, 16, C, 16)
                dist = np.add.reduce(np.abs(v - q[..., None]), axis=1)
                m = np.argmin(dist, axis=2)
                ok = ok & (np.min(dist, axis=2) < H[s][:, k:k + 1] + A[s])
                beta[:, k + 1] = np.take_along_axis(c, m[:, None, :], 1)[:, 0]; live[:, k + 1] = ok
                y = np.maximum(y, np.where(ok[:, None, :], np.take_along_axis(x, beta[:, k + 1:k + 2], 2), 0))
            place = R * np.arange(C) + (np.add.reduce(V[s] * y, axis=1) & (R - 1))
            np.put_along_axis(x, np.repeat(place[:, None, :], 16, axis=1), y, 2)
            last = np.zeros((8, C), np.int64)
            for k in range(K):
                p = np.take_along_axis(beta, last[:, None, :], 1)[:, 0]; dead = ~live[:, k + 1]
                l[:, k] = np.where(dead, ((l[:, k] * p >> 5) + 37 * p + k) & (W - 1), l[:, k])
                u[:, k] = np.where(dead, last - 1, u[:, k])
                last = np.where(dead, last, k + 1)
            deaths[s] = np.count_nonzero(~live)
        A = deaths & 31
    return {"yl": np.stack([gtable(a.reshape(8, -1)) for a in L]).astype(np.float32), "yi": np.stack([gtable(a.reshape(8, -1)) for a in U]).astype(np.float32),
            "yx": X.reshape(N, 128, W).astype(np.float32).astype(BF)}

@@ -1,0 +1,564 @@
+from concourse.mybir import dt, AluOpType, AxisListType, ActivationFunctionType
+
+OP = AluOpType
+ACT = ActivationFunctionType
+NV, NR, PAD, FW = 4, 3, 32, 1264
+BIG = 16777216.0
+ROT = 864
+
+SCRATCH = {}
+
+
+def _decl(where, dtype, names, n, rows=128):
+    for nm in names.split():
+        SCRATCH[nm] = (where, [rows, n], dtype)
+
+
+_decl("sbuf", "bfloat16", "X", 2080)
+_decl("sbuf", "int32", "FA", 2 * FW)
+_decl("sbuf", "float32", "C CT SA RSA onef", 256)
+_decl("sbuf", "uint16", "CTu", 256)
+_decl("sbuf", "bfloat16", "qq yy y0 y01", 256)
+_decl("sbuf", "bfloat16", "Q4 z0 z1 z2 z3", 1024)
+_decl("psum", "float32", "q4ps", 1024)
+_decl("psum", "float32", "CV MS DA DB", 512)
+_decl("sbuf", "float32", "SB RSB", 64)
+_decl("sbuf", "int32", "EXi", 32)
+_decl("sbuf", "uint16", "EXu", 32)
+_decl("sbuf", "int32", "lci upi", 48)
+_decl("sbuf", "int32", "thi", 3, 8)
+_decl("sbuf", "float32", "thf", 3, 8)
+_decl("sbuf", "float32", "tsel", 128, 8)
+_decl("sbuf", "bfloat16", "MK", 256, 1)
+_decl("sbuf", "bfloat16", "MK2", 64, 1)
+_decl("sbuf", "int32", "wti ai ai2 pi pg p15", 1)
+_decl("sbuf", "float32", "wtf cnt af par p8 p15f", 1)
+_decl("sbuf", "float32", "thk Tk", 3)
+_decl("sbuf", "float32", "nc", 8)
+_decl("sbuf", "float32", "D160", 160)
+_decl("sbuf", "bfloat16", "Ev Od", 160)
+_decl("sbuf", "float32", "W", 144)
+_decl("sbuf", "bfloat16", "W65 SW", 144)
+_decl("sbuf", "float32", "I32", 128)
+_decl("sbuf", "bfloat16", "IB oneb", 128)
+_decl("sbuf", "int32", "exi b128 base z32 nn t2 bi rz0 NW0 si sm sa", 16)
+_decl("sbuf", "uint16", "Eu nu bu wu", 16)
+_decl("sbuf", "bfloat16", "eh el bh bl lt", 16)
+_decl("sbuf", "float32", "mone Ep Er Es Mu t1 yo u1 w1 u2 w2 s20 s21 nE sB g1 g2 ga gb px qx df0 x0 a2 pa pb", 16)
+_decl("sbuf", "float32", "n12 P12 LAk rz12", 32)
+_decl("sbuf", "int32", "rk12", 32)
+_decl("sbuf", "int32", "NW", 64)
+_decl("sbuf", "float32", "df xx lvd", 64)
+_decl("sbuf", "bfloat16", "lv Lh Ll", 48)
+_decl("sbuf", "uint16", "Lu yu", 48)
+_decl("sbuf", "float32", "LA LS", 48)
+_decl("sbuf", "int32", "K B", 48)
+_decl("sbuf", "bfloat16", "XL", 768)
+_decl("sbuf", "float32", "land0", 5 * 16)
+_decl("sbuf", "float32", "land1", 5 * 64)
+_decl("sbuf", "float32", "src0", 4 * 16)
+_decl("sbuf", "float32", "src1", 4 * 64)
+
+SEMAPHORES = ["cv", "cs", "cp", "cg", "ls", "dfa", "dfw", "dx", "dy", "dlc", "dup", "dex", "dth", "dwt", "dout"]
+SEMAPHORES += ["ar%d_%d" % (t, k) for t in range(1, 5) for k in range(2)]
+
+
+def rank_program(g, core, T, topo):
+    rank = T.rank_of(core)
+    if rank is None:
+        return
+    n_ranks = len(T.cores)
+    QUEUE = {"v": g.vector, "s": g.scalar, "p": g.tensor, "g": g, "y": g.sync}
+    count = {"v": 0, "s": 0, "p": 0, "g": 0}
+    known = {q: {} for q in QUEUE}
+    snap, lastw, readers, sent = {}, {}, {}, [0]
+
+    def need(q, sem, val):
+        if known[q].get(sem, 0) >= val:
+            return
+        QUEUE[q].wait_ge(T.sem[sem], val)
+        for s_, v_ in snap.get((sem, val), {}).items():
+            if known[q].get(s_, 0) < v_:
+                known[q][s_] = v_
+        known[q][sem] = val
+
+    def before(q, r, w):
+        deps = {}
+
+        def add(d):
+            if deps.get(d[0], 0) < d[1]:
+                deps[d[0]] = d[1]
+        for b in r:
+            if b in lastw:
+                add(lastw[b])
+        for b in w:
+            if b in lastw and not (lastw[b][2] == q and q == "p"):
+                add(lastw[b])
+            for d in readers.get(b, ()):
+                if d[2] != q:
+                    add(d)
+        for sem in sorted(deps, key=lambda s_: -len(snap.get((s_, deps[s_]), {}))):
+            need(q, sem, deps[sem])
+
+    def after(q, sem, val, r, w):
+        d = (sem, val, q)
+        for b in r:
+            readers.setdefault(b, []).append(d)
+        for b in w:
+            lastw[b] = d
+            readers[b] = []
+        snap[(sem, val)] = dict(known[q])
+
+    def op(q, fn, r, w):
+        r, w = r.split(), w.split()
+        before(q, r, w)
+        ins = fn(QUEUE[q])
+        count[q] += 1
+        ins.then_inc(T.sem["c" + q], 1)
+        after(q, "c" + q, count[q], r, w)
+
+    def dma(q, out, in_, sem, total, r, w):
+        r, w = r.split(), w.split()
+        before(q, r, w)
+        QUEUE[q].dma_start(out=out, in_=in_).then_inc(T.sem[sem], 16)
+        after(q, sem, total, r, w)
+
+    def tt(o, a, b, f, r, w):
+        op("v", lambda e: e.tensor_tensor(out=o, in0=a, in1=b, op=f), r, w)
+
+    def ts(o, a, s1, s2, f0, f1, r, w):
+        if s2 is None:
+            op("v", lambda e: e.tensor_scalar(out=o, in0=a, scalar1=s1, scalar2=None, op0=f0), r, w)
+        else:
+            op("v", lambda e: e.tensor_scalar(out=o, in0=a, scalar1=s1, scalar2=s2, op0=f0, op1=f1), r, w)
+
+    def cp(o, a, r, w):
+        op("v", lambda e: e.tensor_copy(out=o, in_=a), r, w)
+
+    def fill(o, c, w):
+        op("v", lambda e: e.memset(o, c), "", w)
+
+    def act(o, a, f, r, w, bias=0.0, scale=1.0):
+        op("s", lambda e: e.activation(out=o, in_=a, func=f, bias=bias, scale=scale), r, w)
+
+    def mms(lst, r, w):
+        def fn(e):
+            ins = None
+            for (o, a, b, st, sp) in lst:
+                ins = e.matmul(out=o, lhsT=a, rhs=b, start=st, stop=sp)
+            return ins
+        op("p", fn, r, w)
+
+    def kk(nm, k):
+        return T[nm][:, 16 * k:16 * k + 16]
+
+    def weave(a, b):
+        for i in range(max(len(a), len(b))):
+            for l in (a, b):
+                if i < len(l) and l[i]:
+                    l[i]()
+
+    Xw = T.X[:, 0:2080]
+
+    dma("y", T.exi[:], T.ex[:], "dex", 16, "", "exi")
+    dma("s", T.lci[:], T.lc[:], "dlc", 16, "", "lci")
+    dma("y", T.X[:, PAD:PAD + 2048], T.xs[:], "dx", 16, "", "X")
+    it = [0]
+
+    def lfa(rows, src, blk):
+        for (a, b, c) in ((0, ROT, 1024), (1024 - ROT, 0, ROT)):
+            q = "sy"[it[0] % 2]
+            it[0] += 1
+            dma(q, T.FA[rows, blk * FW + a:blk * FW + a + c - b], T.fa[src, b:c], "dfa", 288, "", "FA%d" % it[0])
+    lfa(slice(0, 128), slice(0, 128), 0)
+    for G in range(8):
+        o = G ^ 1
+        lfa(slice(16 * G, 16 * G + 16), slice(16 * o, 16 * o + 16), 1)
+    FAtok = " ".join("FA%d" % (i + 1) for i in range(it[0]))
+    dma("y", T.upi[:], T.up[:], "dup", 16, "", "upi")
+    dma("y", T.thi[:], T.th[:], "dth", 16, "", "thi")
+    dma("y", T.wti[:], T.wt[:], "dwt", 16, "", "wti")
+
+    fill(T.onef[:], 1.0, "onef")
+    op("g", lambda e: e.iota(T.pi[:], [[0, 1]], 0, 1), "", "pi")
+
+    def aff(o, a, pat, f, base, cm, r, w):
+        op("g", lambda e: e.affine_select(o, a, pat, f, 0.0, base, cm), r, w)
+
+    def iob(o, pat, base, w):
+        op("g", lambda e: e.iota(o, pat, base, 0, allow_small_or_imprecise_dtypes=True), "", w)
+    aff(T.D160[:], T.onef[:, 0:160], [[-1, 160]], OP.is_equal, 16, 1, "onef", "D160")
+    op("g", lambda e: e.iota(T.EXi[:], [[16, 8], [0, 4]], 0, 0), "", "EXi")
+    aff(T.I32[:], T.onef[:, 0:128], [[-1, 128]], OP.is_equal, 0, 1, "onef", "I32")
+    iob(T.MK[0:1, :], [[0, 16], [4096, 16]], 0, "MK")
+    iob(T.MK2[0:1, :], [[0, 16], [16384, 4]], 8192, "MK2")
+    aff(T.W[:], T.onef[:, 0:144], [[-16, 9], [0, 16]], OP.is_ge, 0, 1, "onef", "W")
+    aff(T.W[:], T.W[:], [[16, 9], [0, 16]], OP.is_ge, 15, -1, "W", "W")
+    aff(T.W[:], T.W[:], [[0, 9], [1, 16]], OP.is_equal, -15, 0, "W", "W")
+    aff(T.RSA[:], T.onef[:], [[0, 16], [1, 16]], OP.is_equal, 0, 0, "onef", "RSA")
+    aff(T.RSB[:], T.onef[:, 0:64], [[0, 16], [1, 4]], OP.is_equal, 0, 0, "onef", "RSB")
+    op("g", lambda e: e.iota(T.b128[:], [[128, 16]], PAD, 0), "", "b128")
+    aff(T.tsel[:], T.onef[0:8, 0:128], [[1, 128]], OP.is_ge, 0, -16, "onef", "tsel")
+    aff(T.tsel[:], T.tsel[:], [[-1, 128]], OP.is_ge, 15, 16, "tsel", "tsel")
+
+    fill(T.FA[:, 1024:FW], 0, "FAx0")
+    fill(T.FA[:, FW + 1024:2 * FW], 0, "FAx1")
+    fill(T.X[:, 0:PAD], 0.0, "Xpad")
+    fill(T.oneb[:], 1.0, "oneb")
+    ts(T.pg[:], T.pi[:], 4, 1, OP.arith_shift_right, OP.bitwise_and, "pi", "pg")
+    ts(T.p15[:], T.pi[:], 15, None, OP.bitwise_and, None, "pi", "p15")
+    cp(T.par[:], T.pg[:], "pg", "par")
+    cp(T.p15f[:], T.p15[:], "p15", "p15f")
+    ts(T.p8[:], T.p15f[:], 8.0, None, OP.mult, None, "p15f", "p8")
+    ts(T.EXu[:], T.EXi[:], T.p15f[:], None, OP.add, None, "EXi p15f", "EXu")
+    REM = [(77 * t) % 8 for t in range(NV)]
+    for t in range(NV):
+        ts(T.nc[:, 2 * t:2 * t + 1], T.par[:], float(FW), float(REM[t]), OP.mult, OP.add, "par", "nc%d" % (2 * t))
+        ts(T.nc[:, 2 * t + 1:2 * t + 2], T.par[:], float(-FW), float(FW + REM[t]), OP.mult, OP.add, "par",
+           "nc%d" % (2 * t + 1))
+    for h, nm in ((1, "Ev"), (0, "Od")):
+        cp(T[nm][:], T.D160[:], "D160", nm)
+        for b in range(10):
+            if b % 2 != h:
+                fill(T[nm][:, 16 * b:16 * b + 16], 0.0, nm)
+
+    MAT = {(0, 0): T.Ev[:, 16:144], (0, 1): T.Ev[:, 0:128], (1, 1): T.Od[:, 16:144], (1, 0): T.Od[:, 32:160]}
+
+    def conv(h, l, bank, a=0, e=16):
+        lst, n = [], (e - a) // 2
+        for gp in range(2):
+            i = 0
+            for part in (h, l):
+                for cc in range(2):
+                    lst.append((T[bank][:, n * gp:n * gp + n], MAT[(gp, cc)], T[part][:, a + cc:e:2], i == 0, i == 3))
+                    i += 1
+        return lst
+
+    def codes(t, w):
+        return T.land1[:, 64 * t:64 * t + 32] if w else T.land0[:, 16 * t:16 * t + 16]
+
+    COL = (slice(0, 16), slice(16, 48))
+
+    def arr_s(t, w):
+        act(T.LA[:, COL[w]], codes(t, w), ACT.Copy, "land%d_%d" % (t, w), "LA%d" % w, bias=1184.0)
+        act(T.Lh[:, COL[w]], T.LA[:, COL[w]], ACT.Copy, "LA%d" % w, "Lh%d" % w)
+
+    def arr_u(t, w):
+        ts(T.Lu[:, COL[w]], codes(t, w), float(PAD), None, OP.add, None, "land%d_%d" % (t, w), "Lu%d" % w)
+
+    def arr_l(w):
+        tt(T.Ll[:, COL[w]], T.LA[:, COL[w]], T.Lh[:, COL[w]], OP.subtract, "LA%d Lh%d" % (w, w), "Ll%d" % w)
+        mms(conv("Lh", "Ll", "MS", 16, 48) if w else conv("Lh", "Ll", "MS"), "Lh%d Ll%d Ev Od" % (w, w), "MS")
+
+    def arr_e(w):
+        if not w:
+            act(T.LS[:, 0:16], T.MS[:, 0:16], ACT.Copy, "", "MS LS0")
+        for k in (1, 2) if w else ():
+            for gp in range(2):
+                act(T.LS[:, 16 * k + 8 * gp:16 * k + 8 * gp + 8], T.MS[:, 16 * gp + 8 * k - 8:16 * gp + 8 * k], ACT.Copy,
+                    "", "MS LS%d" % k)
+
+    def masks1(t):
+        act(T.n12[:], T.land1[:, 64 * t + 32:64 * t + 64], ACT.Relu, "land%d_1" % t, "n12", scale=-1.0)
+        act(T.u1[:], T.n12[:, 0:16], ACT.Copy, "n12", "u1", scale=-BIG, bias=BIG)
+
+    def masks2(t):
+        IN, lk = T.land1[:, 64 * t + 48:64 * t + 64], "land%d_1" % t
+        act(T.s21[:], IN, ACT.Relu, lk, "s21")
+        act(T.u2[:], T.s21[:], ACT.Copy, "s21", "u2", scale=BIG)
+        act(T.a2[:], IN, ACT.Abs, lk, "a2")
+        act(T.s20[:], T.a2[:], ACT.Copy, "a2", "s20", scale=-1.0, bias=1.0)
+        for k in (1, 2):
+            act(T.LAk[:, 16 * k - 16:16 * k], kk("LA", k), ACT.Copy, "LA1", "LAk%d" % k, scale=-32.0, bias=32.0 * k)
+
+    def npart(t, k, bs, btok):
+        es = btok == "Es"
+        w0 = 77 * t - REM[t]
+
+        def nu(gp):
+            return lambda: ts(T.nu[:, gp::2], T.nn[:, 8 * gp:8 * gp + 8], T.nc[:, 2 * t + gp:2 * t + gp + 1], None, OP.add,
+                              None, "nn nc%d" % (2 * t + gp), "nu%d" % gp)
+
+        def ctu(ch):
+            return lambda: cp(T.CTu[:, 64 * ch:64 * ch + 64], T.CT[:, ch::4], "CT", "CTu%d" % ch)
+        return [
+            lambda: tt(T.z32[:], kk("LS", k), bs, OP.mult, "LS%d" % k + (" Es" if es else ""), "z32" + ("" if es else " CV")),
+            lambda: ts(T.nn[:], T.z32[:], 5, 1023, OP.arith_shift_right, OP.bitwise_and, "z32", "nn"),
+            nu(0), nu(1),
+            lambda: ts(T.C[:], T.FA[:, w0:2 * FW].indirect(T.nu[:]), float(PAD), None, OP.add, None,
+                       "nu0 nu1 FAx0 FAx1 " + FAtok, "C"),
+            lambda: op("v", lambda e: e.transpose(out=T.CT[:], in_=T.C[:]), "C", "CT"),
+            ctu(3), ctu(0), ctu(1), ctu(2)]
+
+    def xl(k, halves=(slice(0, 16),)):
+        for s in halves:
+            act(T.XL[:, 256 * k + 16 * s.start:256 * k + 16 * s.stop], Xw.indirect(T.Lu[:, 16 * k + s.start:16 * k + s.stop]),
+                ACT.Copy, "X Xpad Lu%d" % min(k, 1), "XL%d_%d" % (k, s.start))
+
+    HALVES = (slice(0, 8), slice(8, 16))
+
+    def qpart(k, off, otok, halves=(slice(0, 16),)):
+        for s in halves:
+            a, e = 16 * s.start, 16 * s.stop
+            tt(T.qq[:, a:e], Xw.indirect(off[:, s]), T.XL[:, 256 * k + a:256 * k + e], OP.max,
+               "X Xpad %s XL%d_%d" % (otok, k, s.start), "qq1" if a else ("qq0" if e < 256 else "qq0 qq1"))
+        for h in range(2):
+            act(T.Q4[:, 512 * h:512 * h + 512], T.qq[:, 128 * h:128 * h + 128].indirect(T.EXu[:]), ACT.Copy,
+                "qq%d EXu" % h, "Q4%d" % h)
+
+    PLACE = {ch: ("DA", T.DA[:, ch:256:4]) for ch in (0, 1, 3)}
+    PLACE[2] = ("DB", T.DB[:, 0:64])
+
+    def starts():
+        mms([(T.DA[:, 0:256], T.I32[:], T.CT[:], True, False),
+             (T.DA[:, 0:256], T.oneb[0:1, :], T.MK[0:1, :], False, False)], "CT I32 oneb MK", "DA")
+        mms([(T.DB[:, 0:64], T.I32[:], T.CT[:, 2::4], True, False),
+             (T.DB[:, 0:64], T.oneb[0:1, :], T.MK2[0:1, :], False, False)], "CT I32 oneb MK2", "DB")
+
+    def sums(ch, ps, last, r):
+        tok, d = PLACE[ch]
+        mms([(d, T.W65[:, 15 - p:143 - p], T["z%d" % ch][:, p::16], False, last and p == ps[-1]) for p in ps], r + " W65", tok)
+
+    def fused(ch, h, w):
+        a, b, q = (0, 64, "Q40 Q41") if h is None else (32 * h, 32 * h + 32, "Q4%d" % h)
+        tt(T["z%d" % ch][:, 16 * a:16 * b], Xw.indirect(T.CTu[:, 64 * ch + a:64 * ch + b]),
+           T.Q4[:, 16 * a:16 * b], OP.subtract, "X Xpad CTu%d %s" % (ch, q), w)
+
+    def absz(a, tok):
+        act(a, a, ACT.Abs, tok, tok)
+
+    ALL = list(range(16))
+
+    def pair(ch, toks):
+        z = T["z%d" % ch]
+        for s in range(2):
+            absz(z[:, s::2], toks[s])
+            sums(ch, ALL[s::2], s == 1 and ch == 1, toks[s])
+
+    def main():
+        for h in range(2):
+            act(T.z3[:, 512 * h:512 * h + 512], Xw.indirect(T.CTu[:, 192 + 32 * h:224 + 32 * h]), ACT.Copy,
+                "X Xpad CTu3", "z3e%d z3o%d" % (h, h))
+        starts()
+        for h in range(2):
+            mms([(T.q4ps[:, 512 * h:512 * h + 512], T.IB[:], T.Q4[:, 512 * h:512 * h + 512], True, True)], "IB Q4%d" % h, "qp%d" % h)
+        fused(0, 0, "z0e z0o")
+        fused(0, 1, "z0e z0o")
+        pair(0, ("z0e", "z0o"))
+        for h in range(2):
+            z, tok = T.z3[:, 512 * h:512 * h + 512], "z3e%d z3o%d" % (h, h)
+            tt(z, z, T.q4ps[:, 512 * h:512 * h + 512], OP.subtract, tok, tok + " qp%d" % h)
+        pair(3, ("z3e0 z3e1", "z3o0 z3o1"))
+        fused(1, None, "z1e z1o")
+        pair(1, ("z1e", "z1o"))
+        fused(2, 0, "z2a")
+        absz(T.z2[:, 0:512], "z2a")
+        fused(2, 1, "z2e z2o")
+        absz(T.z2[:, 512::2], "z2e")
+        sums(2, ALL[0::2], False, "z2a z2e")
+        absz(T.z2[:, 513::2], "z2o")
+        sums(2, ALL[1::2], True, "z2a z2o")
+
+    def scan(b):
+        op("v", lambda e: e.tensor_tensor_scan(out=T["S" + b][:], data0=T["RS" + b][:], data1=T["D" + b][:, 0:256 if b == "A" else 64],
+                                               initial=BIG, op0=OP.max, op1=OP.min), "RS" + b, "S%s D%s" % (b, b))
+
+    MA, MB = T.SA[:, 15::16], T.SB[:, 3::4]
+
+    def chain(k):
+        tt(T.t1[:], T.Mu[:], MB, OP.min, "Mu SB", "t1")
+        tt(T.t2[:], T.t1[:], T["w%d" % k][:], OP.max, "t1 w%d" % k, "t2")
+        ts(T.bi[:], T.t2[:], 4095, None, OP.bitwise_and, None, "t2", "bi")
+        cp(T.bh[:], T.bi[:], "bi", "bh")
+        cp(T.bu[:], T.bi[:], "bi", "bu")
+        tt(T.bl[:], T.bi[:], T.bh[:], OP.subtract, "bi bh", "bl")
+        mms(conv("bh", "bl", "CV"), "bh bl Ev Od", "CV")
+        qpart(k, T.bu, "bu")
+
+    def keys(k):
+        tc = T.Tk[:, k:k + 1]
+        r = [lambda: tt(kk("K", k), MA, MB, OP.min, "SA SB", "K%d" % k),
+             lambda: ts(kk("B", k), kk("K", k), 4095, None, OP.bitwise_and, None, "K%d" % k, "B%d" % k)]
+        if k == 0:
+            r.append(lambda: ts(kk("lv", 0), kk("K", 0), tc, None, OP.is_lt, None, "K0 Tk", "lv0"))
+        else:
+            r.append(lambda: ts(T.lt[:], kk("K", k), tc, None, OP.is_lt, None, "K%d Tk" % k, "lt"))
+            r.append(lambda: tt(kk("lv", k), T.lt[:], T["g%d" % k][:], OP.mult, "lt g%d" % k, "lv%d" % k))
+        r.append(lambda: tt(T.yo[:], kk("B", k), kk("lv", k), OP.mult, "B%d lv%d" % (k, k), "yo"))
+        r.append(lambda: cp(kk("yu", k), T.yo[:], "yo", "yu%d" % k))
+        return r
+
+    def send(t, w, src, dst_ap):
+        dst = T.cores[(rank + 1) % n_ranks if t < NV - 1 else (rank - t) % n_ranks]
+        before("g", ["src%d_%d" % (t, w)], [])
+        rid, pid = topo.addr(dst, core)
+        ar = "ar%d_%d" % (t + 1, w)
+        g.remote_dma(dst_ap, src, T.sem[ar], T.sem.ls, pid, rid, topo.mask(core, dst))
+        ne = len(topo.engines(core, dst))
+        sent[0] += ne
+        lastw["land%d_%d" % (t + 1, w)] = (ar, ne, "remote")
+
+    def rewire0_pre(t):
+        tt(T.rz0[:], kk("LA", 0), T.Er[:], OP.mult, "LA0 Er", "rz0")
+        ts(T.NW0[:], T.rz0[:], 5, 2047, OP.arith_shift_right, OP.bitwise_and, "rz0", "NW0")
+        tt(T.df0[:], T.NW0[:], T.land0[:, 16 * t:16 * t + 16], OP.subtract, "NW0 land%d_0" % t, "df0")
+
+    def rewire0(t):
+        tt(T.x0[:], T.df0[:], kk("lv", 0), OP.mult, "df0 lv0", "x0")
+        src = T.src0[:, 16 * t:16 * t + 16]
+        tt(src, T.NW0[:], T.x0[:], OP.subtract, "NW0 x0", "src%d_0" % t)
+        send(t, 0, src, T.land0[:, 16 * t + 16:16 * t + 32])
+
+    def rewire1_p1():
+        return [lambda: tt(T.px[:], kk("B", 0), T.Ep[:], OP.subtract, "B0 Ep", "px"),
+                lambda: tt(T.px[:], T.px[:], kk("lv", 0), OP.mult, "px lv0", "px"),
+                lambda: ts(T.NW[:, 32:48], kk("lv", 0), -1.0, None, OP.add, None, "lv0", "NWp1"),
+                lambda: tt(T.P12[:, 0:16], T.px[:], T.Ep[:], OP.add, "px Ep", "P1")]
+
+    def rewire1_pre(t):
+        return [lambda: tt(T.qx[:], kk("B", 1), T.P12[:, 0:16], OP.subtract, "B1 P1", "qx"),
+                lambda: tt(T.qx[:], T.qx[:], kk("lv", 1), OP.mult, "qx lv1", "qx"),
+                lambda: tt(T.P12[:, 16:32], T.qx[:], T.P12[:, 0:16], OP.add, "qx P1", "P2"),
+                lambda: tt(T.NW[:, 48:64], T.pa[:], T.pb[:], OP.max, "pa pb", "NWp2"),
+                lambda: tt(T.rz12[:], T.LA[:, 16:48], T.P12[:], OP.mult, "LA1 P1 P2", "rz12"),
+                lambda: tt(T.rk12[:], T.rz12[:], T.LAk[:], OP.add, "rz12 LAk1 LAk2", "rk12"),
+                lambda: ts(T.NW[:, 0:32], T.rk12[:], 5, 2047, OP.arith_shift_right, OP.bitwise_and, "rk12", "NWl"),
+                lambda: tt(T.df[:], T.NW[:], T.land1[:, 64 * t:64 * t + 64], OP.subtract, "NWl NWp1 NWp2 land%d_1" % t, "df")]
+
+    def rewire1(t):
+        src = T.src1[:, 64 * t:64 * t + 64]
+        return [lambda: tt(T.xx[:], T.df[:], T.lvd[:], OP.mult, "df lvd0 lvd1", "xx"),
+                lambda: tt(src, T.NW[:], T.xx[:], OP.subtract, "NWl NWp1 NWp2 xx", "src%d_1" % t),
+                lambda: send(t, 1, src, T.land1[:, 64 * t + 64:64 * t + 128])]
+
+    def thresholds():
+        return [lambda: op("v", lambda e: e.tensor_reduce(out=T.cnt[:], in_=T.CV[:, 0:48], axis=AxisListType.X, op=OP.add), "", "cnt CV"),
+                lambda: ts(T.ai[:], T.cnt[:], -1.0, 6144.0, OP.mult, OP.add, "cnt", "ai"),
+                lambda: ts(T.ai2[:], T.ai[:], 31, None, OP.bitwise_and, None, "ai", "ai2"),
+                lambda: ts(T.af[:], T.ai2[:], 65536.0, None, OP.mult, None, "ai2", "af"),
+                lambda: ts(T.Tk[:], T.thk[:], T.af[:], None, OP.add, None, "thk af", "Tk")]
+
+    ts(T.Ep[:], T.exi[:], float(PAD), None, OP.add, None, "exi", "Ep")
+    cp(T.eh[:], T.Ep[:], "Ep", "eh")
+    tt(T.el[:], T.Ep[:], T.eh[:], OP.subtract, "Ep eh", "el")
+    mms(conv("eh", "el", "CV"), "eh el Ev Od", "CV")
+    act(T.Es[:], T.CV[:, 0:16], ACT.Copy, "", "CV Es")
+    cp(T.land0[:, 0:16], T.lci[:, 0:16], "lci", "land0_0")
+    cp(T.Eu[:], T.Ep[:], "Ep", "Eu")
+    arr_s(0, 0)
+    arr_u(0, 0)
+    arr_l(0)
+    arr_e(0)
+    xl(0, HALVES)
+    cp(T.Er[:], T.exi[:], "exi", "Er")
+    ts(T.W65[:], T.W[:], 65536.0, None, OP.mult, None, "W", "W65")
+    cp(T.IB[:], T.I32[:], "I32", "IB")
+    ts(T.RSA[:], T.RSA[:], BIG, None, OP.mult, None, "RSA", "RSA")
+    ts(T.RSB[:], T.RSB[:], BIG, None, OP.mult, None, "RSB", "RSB")
+    fill(T.MK[0:1, 2::4], BIG, "MK")
+    np_ = npart(0, 0, T.Es[:], "Es")
+    weave(np_[0:4], [])
+    qpart(0, T.Eu, "Eu", HALVES)
+    cp(T.land1[:, 0:32], T.lci[:, 16:48], "lci", "land0_1")
+    ts(T.tsel[:], T.tsel[:], 65536.0, None, OP.mult, None, "tsel", "tsel")
+    ts(T.base[:], T.b128[:], T.p8[:], None, OP.add, None, "b128 p8", "base")
+    fill(T.mone[:], -1.0, "mone")
+    dma("y", T.yi[:, 0:16], T.mone[:], "dout", 64, "mone", "yi0")
+    weave(np_[4:], [])
+    cp(T.land1[:, 32:64], T.upi[:, 16:48], "upi", "land0_1")
+    cp(T.thf[:], T.thi[:], "thi", "thf")
+    cp(T.wtf[:], T.wti[:], "wti", "wtf")
+    ts(T.SW[:], T.W[:], T.wtf[:], None, OP.mult, None, "W wtf", "SW")
+    for b in range(2):
+        dma("y", T.FA[:, b * FW + 1024:(b + 1) * FW], T.FA[:, b * FW:b * FW + FW - 1024], "dfw", 32, FAtok, "FAx%d" % b)
+
+    for t in range(NV):
+        more = t < NV - 1
+        main()
+        if t == 0:
+            mms([(T.MS[:, 0:3], T.tsel[:], T.thf[:], True, True)], "tsel thf", "MS")
+            act(T.thk[:], T.MS[:, 0:3], ACT.Copy, "", "MS thk")
+            act(T.Tk[:], T.thk[:], ACT.Copy, "thk", "Tk")
+        arr_u(t, 1)
+        arr_s(t, 1)
+        masks1(t)
+        xl(1)
+        rewire0_pre(t)
+        scan("A")
+        arr_l(1)
+        masks2(t)
+        arr_e(1)
+        tt(T.w1[:], T.n12[:, 0:16], T.Ep[:], OP.mult, "n12 Ep", "w1")
+        tt(T.Mu[:], MA, T.u1[:], OP.min, "SA u1", "Mu")
+        tt(T.nE[:], T.n12[:, 16:32], T.Ep[:], OP.mult, "n12 Ep", "nE")
+        scan("B")
+        chain(1)
+        ks = keys(0)
+        weave(ks[0:2], [])
+        weave(npart(t, 1, T.CV[:, 0:16], "CV"), ks[2:])
+        main()
+        xl(2)
+        act(T.y0[:], Xw.indirect(kk("yu", 0)), ACT.Copy, "X Xpad yu0", "y0")
+        rewire0(t)
+        tt(T.sB[:], T.s20[:], kk("B", 0), OP.mult, "s20 B0", "sB")
+        scan("A")
+        weave([lambda: tt(T.w2[:], T.sB[:], T.nE[:], OP.add, "sB nE", "w2"),
+               lambda: tt(T.Mu[:], MA, T.u2[:], OP.min, "SA u2", "Mu"),
+               lambda: tt(T.g1[:], T.n12[:, 0:16], kk("lv", 0), OP.max, "n12 lv0", "g1"),
+               lambda: tt(T.ga[:], T.s20[:], kk("lv", 0), OP.mult, "s20 lv0", "ga")], rewire1_p1())
+        scan("B")
+        chain(2)
+        ks = keys(1)
+        weave(ks[0:2], [])
+        weave(npart(t, 2, T.CV[:, 0:16], "CV"), ks[2:])
+        main()
+        if more:
+            arr_u(t + 1, 0)
+            arr_s(t + 1, 0)
+        act(T.pb[:], kk("lv", 0), ACT.Copy, "lv0", "pb", bias=-1.0)
+        act(T.pa[:], kk("lv", 1), ACT.Copy, "lv1", "pa", scale=2.0, bias=-1.0)
+        tt(T.gb[:], T.s21[:], kk("lv", 1), OP.mult, "s21 lv1", "gb")
+        tt(T.ga[:], T.ga[:], T.n12[:, 16:32], OP.max, "ga n12", "ga")
+        tt(T.y01[:], Xw.indirect(kk("yu", 1)), T.y0[:], OP.max, "X Xpad yu1 y0", "y01")
+        scan("A")
+        weave([lambda: tt(T.g2[:], T.ga[:], T.gb[:], OP.max, "ga gb", "g2"),
+               (lambda: (arr_l(0), arr_e(0))) if more else None], rewire1_pre(t))
+        scan("B")
+        np_ = npart(t + 1, 0, T.Es[:], "Es") if more else []
+        weave(keys(2), [None] * 3 + np_[0:4])
+        for h in range(2):
+            act(T.lvd[:, 32 * h:32 * h + 32], T.lv[:, 16:48], ACT.Copy, "lv1 lv2", "lvd%d" % h)
+        tt(T.yy[:], Xw.indirect(kk("yu", 2)), T.y01[:], OP.max, "X Xpad yu2 y01", "yy")
+        mms([(T.CV[:, 0:16], T.SW[:, 15 - p:143 - p], T.yy[:, p::16], p == 0, p == 15) for p in ALL], "SW yy", "CV")
+        weave(np_[4:], [])
+        put = [lambda: cp(T.si[:], T.CV[:, 0:16], "", "si CV"),
+               lambda: ts(T.sm[:], T.si[:], 7, None, OP.bitwise_and, None, "si", "sm"),
+               lambda: tt(T.sa[:], T.sm[:], T.base[:], OP.add, "sm base", "sa")]
+        if more:
+            put.append(lambda: cp(T.wu[:], T.sa[:], "sa", "wu"))
+            weave(put, rewire1(t))
+            op("v", lambda e: e.tensor_copy(out=Xw.indirect(T.wu[:]), in_=T.yy[:]), "wu yy", "X Xpad")
+            xl(0, HALVES)
+            mms([(T.CV[:, 0:48], T.oneb[:], T.lv[:], True, True)], "oneb lv0 lv1 lv2", "CV")
+            th = thresholds()
+            weave(th[0:3], [])
+            qpart(0, T.Eu, "Eu", HALVES)
+            weave(th[3:], [])
+        else:
+            weave(rewire1(t), put)
+            M = PAD + 1024
+            cp(T.wu[:, 0:8], T.sa[:, 0:8], "sa", "wu0")
+            ts(T.wu[:, 8:16], T.sa[:, 8:16], float(-M), None, OP.add, None, "sa", "wu1")
+            op("v", lambda e: e.tensor_copy(out=T.X[:, 0:M].indirect(T.wu[:, 0:8]), in_=T.yy[:, 0:128]), "wu0 yy X", "Xpad")
+            op("v", lambda e: e.tensor_copy(out=T.X[:, M:M + 1024].indirect(T.wu[:, 8:16]), in_=T.yy[:, 128:256]), "wu1 yy", "X")
+            dma("s", T.yx[:, 0:1024], T.X[:, PAD:M], "dy", 32, "Xpad", "yxo0")
+            dma("s", T.yx[:, 1024:2048], T.X[:, M:M + 1024], "dy", 32, "X", "yxo1")
+
+    dma("y", T.yl[:, 0:16], T.land0[:, 16 * NV:16 * NV + 16], "dout", 64, "land%d_0" % NV, "ylo0")
+    dma("y", T.yl[:, 16:48], T.land1[:, 64 * NV:64 * NV + 32], "dout", 64, "land%d_1" % NV, "ylo1")
+    dma("y", T.yi[:, 16:48], T.land1[:, 64 * NV + 32:64 * NV + 64], "dout", 64, "land%d_1" % NV, "yio1")
+    need("g", "dout", 64)
+    need("g", "dy", 32)
+    need("g", "ls", sent[0])
+    for q in ("v", "s", "p", "g"):
+        need("g", "c" + q, count[q])

@@ -3,8 +3,10 @@ from concourse.mybir import dt, AluOpType, AxisListType, ActivationFunctionType
 OP = AluOpType
 ACT = ActivationFunctionType
 NV, NR, PAD, FW = 4, 3, 32, 1264
-BIG = 16777216.0
 ROT = 864
+CHUNKS = [("A", 0, 4), ("D", 4, 8), ("A", 8, 10), ("D", 10, 13), ("D", 13, 16)]
+QREP, BIG = 4, 2.0 ** 25
+LOW = 240 * 65536.0
 
 SCRATCH = {}
 
@@ -15,52 +17,111 @@ def _decl(where, dtype, names, n, rows=128):
 
 
 _decl("sbuf", "bfloat16", "X", 2080)
-_decl("sbuf", "int32", "FA", 2 * FW)
-_decl("sbuf", "float32", "C CT SA RSA onef", 256)
+_decl("sbuf", "int32", "FA", FW)
+_decl("sbuf", "float16", "C CT", 256)
 _decl("sbuf", "uint16", "CTu", 256)
-_decl("sbuf", "bfloat16", "qq yy y0 y01", 256)
-_decl("sbuf", "bfloat16", "Q4 z0 z1 z2 z3", 1024)
-_decl("psum", "float32", "q4ps", 1024)
-_decl("psum", "float32", "CV MS DA DB", 512)
-_decl("sbuf", "float32", "SB RSB", 64)
-_decl("sbuf", "int32", "EXi", 32)
-_decl("sbuf", "uint16", "EXu", 32)
+_decl("sbuf", "bfloat16", "Q0 Q1", 128 * QREP)
+_decl("sbuf", "bfloat16", "Z0 Z1 Y0 Y1", 2048)
+_decl("sbuf", "bfloat16", "XL", 768)
+_decl("sbuf", "bfloat16", "yy y0 y01", 256)
+_decl("psum", "float32", "KB0 KB1 KN PB MS D0 D1 D2", 512)
+_decl("sbuf", "float32", "SA0 SA1 KX RS pm", 128)
+_decl("sbuf", "float32", "onef D160", 160)
+_decl("sbuf", "float16", "Ev Od", 160)
+_decl("sbuf", "float16", "I16", 128)
+_decl("sbuf", "bfloat16", "IB NI oneb MK SX", 128)
+_decl("sbuf", "float32", "W", 8)
+_decl("sbuf", "bfloat16", "W1 W2 Wb SW", 8)
+_decl("sbuf", "int32", "e15 e1", 8)
+_decl("sbuf", "uint16", "e15u e1u", 8)
+_decl("sbuf", "float16", "base", 16)
 _decl("sbuf", "int32", "lci upi", 48)
 _decl("sbuf", "int32", "thi", 3, 8)
 _decl("sbuf", "float32", "thf", 3, 8)
 _decl("sbuf", "float32", "tsel", 128, 8)
-_decl("sbuf", "bfloat16", "MK", 256, 1)
-_decl("sbuf", "bfloat16", "MK2", 64, 1)
 _decl("sbuf", "int32", "wti ai ai2 pi pg p15", 1)
-_decl("sbuf", "float32", "wtf cnt af par p8 p15f", 1)
+_decl("sbuf", "float32", "wtf cnt af par npar p8 p15f c4k", 1)
 _decl("sbuf", "float32", "thk Tk", 3)
-_decl("sbuf", "float32", "nc", 8)
-_decl("sbuf", "float32", "D160", 160)
-_decl("sbuf", "bfloat16", "Ev Od", 160)
-_decl("sbuf", "float32", "W", 144)
-_decl("sbuf", "bfloat16", "W65 SW", 144)
-_decl("sbuf", "float32", "I32", 128)
-_decl("sbuf", "bfloat16", "IB oneb", 128)
-_decl("sbuf", "int32", "exi b128 base z32 nn t2 bi rz0 NW0 si sm sa", 16)
+_decl("sbuf", "int32", "exi b128 z32 nn t1 bi si sm rz0", 16)
 _decl("sbuf", "uint16", "Eu nu bu wu", 16)
-_decl("sbuf", "bfloat16", "eh el bh bl lt", 16)
-_decl("sbuf", "float32", "mone Ep Er Es Mu t1 yo u1 w1 u2 w2 s20 s21 nE sB g1 g2 ga gb px qx df0 x0 a2 pa pb", 16)
-_decl("sbuf", "float32", "n12 P12 LAk rz12", 32)
-_decl("sbuf", "int32", "rk12", 32)
-_decl("sbuf", "int32", "NW", 64)
-_decl("sbuf", "float32", "df xx lvd", 64)
-_decl("sbuf", "bfloat16", "lv Lh Ll", 48)
+_decl("sbuf", "float32", "mone Ep nEp u1 w1 u2 w2 n2 a2 nE sB g1 Tg1 Tg2 g2 px pa", 16)
+_decl("sbuf", "float32", "s2 dd sd P Pu rz K32", 32)
+_decl("sbuf", "int32", "rk", 32)
 _decl("sbuf", "uint16", "Lu yu", 48)
-_decl("sbuf", "float32", "LA LS", 48)
+_decl("sbuf", "float32", "LA cdum", 48)
 _decl("sbuf", "int32", "K B", 48)
-_decl("sbuf", "bfloat16", "XL", 768)
-_decl("sbuf", "float32", "land0", 5 * 16)
-_decl("sbuf", "float32", "land1", 5 * 64)
-_decl("sbuf", "float32", "src0", 4 * 16)
-_decl("sbuf", "float32", "src1", 4 * 64)
+_decl("sbuf", "int32", "NW", 80)
+_decl("sbuf", "float32", "df xx", 80)
+_decl("sbuf", "bfloat16", "lv", 80)
+_decl("sbuf", "float32", "land", 5 * 80)
+_decl("sbuf", "float32", "src", 4 * 80)
 
-SEMAPHORES = ["cv", "cs", "cp", "cg", "ls", "dfa", "dfw", "dx", "dy", "dlc", "dup", "dex", "dth", "dwt", "dout"]
-SEMAPHORES += ["ar%d_%d" % (t, k) for t in range(1, 5) for k in range(2)]
+SEMAPHORES = ["cv", "cs", "cp", "cg", "ls", "dfa", "dfw", "dx", "dy0", "dy1", "dlc", "dup", "dex", "dth", "dwt"]
+SEMAPHORES += ["do%d" % i for i in range(6)]
+SEMAPHORES += ["ar%d%s" % (t, k) for t in range(1, 5) for k in "ABC"]
+
+CYC, PEC, GATHER, SCATTER, HOP, CROSS, FAR = 0.00088, 0.00060, 1.56, 3.8, 0.12, 0.27, 5.0
+AHEAD, ROUNDS = 40.0, 4
+ORDER = []
+
+
+def issue_order(jobs):
+    n = len(jobs)
+    pred, succ = [set() for _ in range(n)], [[] for _ in range(n)]
+    lastw, readers = {}, {}
+    for i, (q, fn, r, w, busy, late, lazy) in enumerate(jobs):
+        for b in r:
+            if b in lastw:
+                pred[i].add(lastw[b])
+        for b in w:
+            if b in lastw:
+                pred[i].add(lastw[b])
+            pred[i].update(readers.get(b, ()))
+        pred[i].discard(i)
+        for b in r:
+            readers.setdefault(b, []).append(i)
+        for b in w:
+            lastw[b], readers[b] = i, []
+        for j in pred[i]:
+            succ[j].append(i)
+    place = list(range(n))
+    for i in range(n - 1, -1, -1):
+        if jobs[i][6] and succ[i]:
+            place[i] = min(place[j] for j in succ[i]) - AHEAD * (jobs[i][4] + jobs[i][5] + HOP)
+
+    def gap(i, j):
+        return jobs[i][5] + (CROSS if jobs[i][0] != jobs[j][0] else 0.0 if jobs[i][0] == "p" else HOP)
+
+    def lay(key, before_, after_, back):
+        at, taken, left = [0.0] * n, {}, [len(p) for p in before_]
+        ready = sorted((key[i], i) for i in range(n) if not left[i])
+        while ready:
+            i = ready.pop(0)[1]
+            t = max([at[j] + jobs[j][4] + (gap(i, j) if back else gap(j, i)) for j in before_[i]] + [jobs[i][5] if back else 0.0])
+            line = taken.setdefault(jobs[i][0], [])
+            k = len(line)
+            while k and line[k - 1][1] > t:
+                k -= 1
+            while k < len(line) and line[k][0] < t + jobs[i][4]:
+                t = max(t, line[k][1])
+                k += 1
+            line.insert(k, (t, t + jobs[i][4]))
+            at[i] = t
+            for j in after_[i]:
+                left[j] -= 1
+                if not left[j]:
+                    ready.append((key[j], j))
+            ready.sort()
+        return at
+    best, key = None, place
+    for _ in range(ROUNDS):
+        at = lay(key, pred, succ, False)
+        end = max(at[i] + jobs[i][4] + jobs[i][5] for i in range(n))
+        if best is None or end < best[0]:
+            best = (end, at)
+        late = lay([-at[i] - jobs[i][4] for i in range(n)], succ, pred, True)
+        key = [-late[i] - jobs[i][4] for i in range(n)]
+    return sorted(range(n), key=lambda i: (best[1][i], i))
 
 
 def rank_program(g, core, T, topo):
@@ -71,7 +132,7 @@ def rank_program(g, core, T, topo):
     QUEUE = {"v": g.vector, "s": g.scalar, "p": g.tensor, "g": g, "y": g.sync}
     count = {"v": 0, "s": 0, "p": 0, "g": 0}
     known = {q: {} for q in QUEUE}
-    snap, lastw, readers, sent = {}, {}, {}, [0]
+    snap, lastw, readers, sent, jobs, lazy = {}, {}, {}, [0], [], [False]
 
     def need(q, sem, val):
         if known[q].get(sem, 0) >= val:
@@ -95,8 +156,7 @@ def rank_program(g, core, T, topo):
             if b in lastw and not (lastw[b][2] == q and q == "p"):
                 add(lastw[b])
             for d in readers.get(b, ()):
-                if d[2] != q:
-                    add(d)
+                add(d)
         for sem in sorted(deps, key=lambda s_: -len(snap.get((s_, deps[s_]), {}))):
             need(q, sem, deps[sem])
 
@@ -109,456 +169,394 @@ def rank_program(g, core, T, topo):
             readers[b] = []
         snap[(sem, val)] = dict(known[q])
 
-    def op(q, fn, r, w):
+    def op(q, fn, r, w, busy):
         r, w = r.split(), w.split()
-        before(q, r, w)
-        ins = fn(QUEUE[q])
-        count[q] += 1
-        ins.then_inc(T.sem["c" + q], 1)
-        after(q, "c" + q, count[q], r, w)
 
-    def dma(q, out, in_, sem, total, r, w):
+        def issue():
+            before(q, r, w)
+            ins = fn(QUEUE[q])
+            count[q] += 1
+            ins.then_inc(T.sem["c" + q], 1)
+            after(q, "c" + q, count[q], r, w)
+        jobs.append((q, issue, r, w, busy, 0.0, lazy[0]))
+
+    def dma(q, out, in_, sem, total, r, w, late=2.0):
         r, w = r.split(), w.split()
-        before(q, r, w)
-        QUEUE[q].dma_start(out=out, in_=in_).then_inc(T.sem[sem], 16)
-        after(q, sem, total, r, w)
 
-    def tt(o, a, b, f, r, w):
-        op("v", lambda e: e.tensor_tensor(out=o, in0=a, in1=b, op=f), r, w)
+        def issue():
+            before(q, r, w)
+            QUEUE[q].dma_start(out=out, in_=in_).then_inc(T.sem[sem], 16)
+            after(q, sem, total, r, w)
+        jobs.append((q, issue, r, w, 0.06, late, lazy[0]))
 
-    def ts(o, a, s1, s2, f0, f1, r, w):
+    def cyc(n):
+        return max(n, 64) * CYC
+
+    def gat(n):
+        return 0.06 + n * GATHER * CYC
+
+    def tt(o, a, b, f, r, w, c=cyc(0)):
+        op("v", lambda e: e.tensor_tensor(out=o, in0=a, in1=b, op=f), r, w, c)
+
+    def ts(o, a, s1, s2, f0, f1, r, w, c=cyc(0)):
         if s2 is None:
-            op("v", lambda e: e.tensor_scalar(out=o, in0=a, scalar1=s1, scalar2=None, op0=f0), r, w)
+            op("v", lambda e: e.tensor_scalar(out=o, in0=a, scalar1=s1, scalar2=None, op0=f0), r, w, c)
         else:
-            op("v", lambda e: e.tensor_scalar(out=o, in0=a, scalar1=s1, scalar2=s2, op0=f0, op1=f1), r, w)
+            op("v", lambda e: e.tensor_scalar(out=o, in0=a, scalar1=s1, scalar2=s2, op0=f0, op1=f1), r, w, c)
 
-    def cp(o, a, r, w):
-        op("v", lambda e: e.tensor_copy(out=o, in_=a), r, w)
+    def cp(o, a, r, w, c=cyc(0)):
+        op("v", lambda e: e.tensor_copy(out=o, in_=a), r, w, c)
 
-    def fill(o, c, w):
-        op("v", lambda e: e.memset(o, c), "", w)
+    def fill(o, v, w, c=cyc(0)):
+        op("v", lambda e: e.memset(o, v), "", w, c)
 
-    def act(o, a, f, r, w, bias=0.0, scale=1.0):
-        op("s", lambda e: e.activation(out=o, in_=a, func=f, bias=bias, scale=scale), r, w)
+    def act(o, a, f, r, w, c=cyc(0), bias=0.0, scale=1.0):
+        op("s", lambda e: e.activation(out=o, in_=a, func=f, bias=bias, scale=scale), r, w, c)
 
-    def mms(lst, r, w):
+    def mms(lst, r, w, n=64):
         def fn(e):
             ins = None
             for (o, a, b, st, sp) in lst:
                 ins = e.matmul(out=o, lhsT=a, rhs=b, start=st, stop=sp)
             return ins
-        op("p", fn, r, w)
+        op("p", fn, r, w, len(lst) * max(n, 64) * PEC)
 
-    def kk(nm, k):
-        return T[nm][:, 16 * k:16 * k + 16]
+    def aff(o, a, pat, f, base, cm, r, w, n):
+        op("g", lambda e: e.affine_select(o, a, pat, f, 0.0, base, cm), r, w, 0.19 + 2 * n * CYC)
 
-    def weave(a, b):
-        for i in range(max(len(a), len(b))):
-            for l in (a, b):
-                if i < len(l) and l[i]:
-                    l[i]()
+    def iota(o, pat, base, cm, w, n, small=False):
+        if small:
+            op("g", lambda e: e.iota(o, pat, base, cm, allow_small_or_imprecise_dtypes=True), "", w, 0.15 + 2 * n * CYC)
+        else:
+            op("g", lambda e: e.iota(o, pat, base, cm), "", w, 0.15 + 2 * n * CYC)
 
-    Xw = T.X[:, 0:2080]
+    def col(nm, k, h=None):
+        a = 16 * k
+        return T[nm][:, a:a + 16] if h is None else T[nm][:, a + 8 * h:a + 8 * h + 8]
+
+    def toks(s, h):
+        return " ".join(x.replace("%", str(u)) for x in s.split() for u in ((0, 1) if h is None else (h,)))
+
+    Xw, XT = T.X[:, 0:2080], "X0 X1 Xpad"
 
     dma("y", T.exi[:], T.ex[:], "dex", 16, "", "exi")
     dma("s", T.lci[:], T.lc[:], "dlc", 16, "", "lci")
-    dma("y", T.X[:, PAD:PAD + 2048], T.xs[:], "dx", 16, "", "X")
-    it = [0]
+    dma("y", T.FA[:, 1024 - ROT:1024], T.fa[:, 0:ROT], "dfa", 32, "", "FA1", 3.5)
+    dma("s", T.FA[:, 0:1024 - ROT], T.fa[:, ROT:1024], "dfa", 32, "", "FA2", 3.5)
+    dma("s", T.X[:, PAD:PAD + 2048], T.xs[:], "dx", 16, "", "X0 X1", 4.5)
+    lazy[0] = True
+    dma("y", T.upi[:], T.up[:], "dup", 16, "FA1", "upi", 3.0)
+    dma("y", T.thi[:], T.th[:], "dth", 16, "FA1", "thi", 3.0)
+    dma("y", T.wti[:], T.wt[:], "dwt", 16, "FA1", "wti", 3.0)
 
-    def lfa(rows, src, blk):
-        for (a, b, c) in ((0, ROT, 1024), (1024 - ROT, 0, ROT)):
-            q = "sy"[it[0] % 2]
-            it[0] += 1
-            dma(q, T.FA[rows, blk * FW + a:blk * FW + a + c - b], T.fa[src, b:c], "dfa", 288, "", "FA%d" % it[0])
-    lfa(slice(0, 128), slice(0, 128), 0)
-    for G in range(8):
-        o = G ^ 1
-        lfa(slice(16 * G, 16 * G + 16), slice(16 * o, 16 * o + 16), 1)
-    FAtok = " ".join("FA%d" % (i + 1) for i in range(it[0]))
-    dma("y", T.upi[:], T.up[:], "dup", 16, "", "upi")
-    dma("y", T.thi[:], T.th[:], "dth", 16, "", "thi")
-    dma("y", T.wti[:], T.wt[:], "dwt", 16, "", "wti")
+    fill(T.onef[:], 1.0, "onef", cyc(160))
+    iota(T.pi[:], [[0, 1]], 0, 1, "pi", 1)
+    aff(T.D160[:], T.onef[:], [[-1, 160]], OP.is_equal, 16, 1, "onef", "D160", 160)
+    fill(T.MK[:], 0.0, "MK")
+    iota(T.MK[0:1, :], [[0, 8], [4096, 16]], 0, 0, "MK", 128, True)
+    fill(T.MK[32:33, :], float(PAD), "MK")
+    fill(T.MK[64:65, :], -LOW, "MK")
+    aff(T.W[:], T.onef[:, 0:8], [[-16, 8]], OP.is_ge, 0, 1, "onef", "W", 8)
+    aff(T.W[:], T.W[:], [[16, 8]], OP.is_ge, 15, -1, "W", "W", 8)
+    iota(T.pm[:], [[0, 8], [1, 16]], 0, 0, "pm", 128, True)
+    iota(T.e15[:], [[16, 8]], 15, 0, "e15", 8)
+    iota(T.e1[:], [[1, 8]], 0, 0, "e1", 8)
+    iota(T.b128[:], [[-PAD, 2], [128, 8]], PAD, 0, "b128", 16)
+    iota(T.K32[:], [[32, 2], [0, 16]], 32, 0, "K32", 32, True)
+    aff(T.tsel[:], T.onef[0:8, 0:128], [[1, 128]], OP.is_ge, 0, -16, "onef", "tsel", 128)
+    aff(T.tsel[:], T.tsel[:], [[-1, 128]], OP.is_ge, 15, 16, "tsel", "tsel", 128)
 
-    fill(T.onef[:], 1.0, "onef")
-    op("g", lambda e: e.iota(T.pi[:], [[0, 1]], 0, 1), "", "pi")
-
-    def aff(o, a, pat, f, base, cm, r, w):
-        op("g", lambda e: e.affine_select(o, a, pat, f, 0.0, base, cm), r, w)
-
-    def iob(o, pat, base, w):
-        op("g", lambda e: e.iota(o, pat, base, 0, allow_small_or_imprecise_dtypes=True), "", w)
-    aff(T.D160[:], T.onef[:, 0:160], [[-1, 160]], OP.is_equal, 16, 1, "onef", "D160")
-    op("g", lambda e: e.iota(T.EXi[:], [[16, 8], [0, 4]], 0, 0), "", "EXi")
-    aff(T.I32[:], T.onef[:, 0:128], [[-1, 128]], OP.is_equal, 0, 1, "onef", "I32")
-    iob(T.MK[0:1, :], [[0, 16], [4096, 16]], 0, "MK")
-    iob(T.MK2[0:1, :], [[0, 16], [16384, 4]], 8192, "MK2")
-    aff(T.W[:], T.onef[:, 0:144], [[-16, 9], [0, 16]], OP.is_ge, 0, 1, "onef", "W")
-    aff(T.W[:], T.W[:], [[16, 9], [0, 16]], OP.is_ge, 15, -1, "W", "W")
-    aff(T.W[:], T.W[:], [[0, 9], [1, 16]], OP.is_equal, -15, 0, "W", "W")
-    aff(T.RSA[:], T.onef[:], [[0, 16], [1, 16]], OP.is_equal, 0, 0, "onef", "RSA")
-    aff(T.RSB[:], T.onef[:, 0:64], [[0, 16], [1, 4]], OP.is_equal, 0, 0, "onef", "RSB")
-    op("g", lambda e: e.iota(T.b128[:], [[128, 16]], PAD, 0), "", "b128")
-    aff(T.tsel[:], T.onef[0:8, 0:128], [[1, 128]], OP.is_ge, 0, -16, "onef", "tsel")
-    aff(T.tsel[:], T.tsel[:], [[-1, 128]], OP.is_ge, 15, 16, "tsel", "tsel")
-
-    fill(T.FA[:, 1024:FW], 0, "FAx0")
-    fill(T.FA[:, FW + 1024:2 * FW], 0, "FAx1")
+    fill(T.FA[:, 1024:FW], 0, "FAx", cyc(240))
     fill(T.X[:, 0:PAD], 0.0, "Xpad")
     fill(T.oneb[:], 1.0, "oneb")
+    fill(T.mone[:], -1.0, "mone")
+    fill(T.c4k[:], 4096.0, "c4k")
     ts(T.pg[:], T.pi[:], 4, 1, OP.arith_shift_right, OP.bitwise_and, "pi", "pg")
     ts(T.p15[:], T.pi[:], 15, None, OP.bitwise_and, None, "pi", "p15")
     cp(T.par[:], T.pg[:], "pg", "par")
+    ts(T.npar[:], T.pg[:], -1.0, 1.0, OP.mult, OP.add, "pg", "npar")
+    ts(T.p8[:], T.p15[:], 8.0, None, OP.mult, None, "p15", "p8")
+    ts(T.Ev[:], T.D160[:], T.npar[:], None, OP.mult, None, "D160 npar", "Ev", cyc(160))
+    ts(T.Od[:], T.D160[:], T.par[:], None, OP.mult, None, "D160 par", "Od", cyc(160))
+    act(T.IB[:], T.D160[:, 16:144], ACT.Copy, "D160", "IB", cyc(128))
+    act(T.NI[:], T.D160[:, 16:144], ACT.Copy, "D160", "NI", cyc(128), scale=-1.0)
+    for nm, f in (("W1", 65536.0), ("W2", -131072.0), ("Wb", 1.0)):
+        act(T[nm][:], T.W[:], ACT.Copy, "W", nm, scale=f)
+    cp(T.I16[:], T.D160[:, 16:144], "D160", "I16", cyc(128))
     cp(T.p15f[:], T.p15[:], "p15", "p15f")
-    ts(T.p8[:], T.p15f[:], 8.0, None, OP.mult, None, "p15f", "p8")
-    ts(T.EXu[:], T.EXi[:], T.p15f[:], None, OP.add, None, "EXi p15f", "EXu")
-    REM = [(77 * t) % 8 for t in range(NV)]
-    for t in range(NV):
-        ts(T.nc[:, 2 * t:2 * t + 1], T.par[:], float(FW), float(REM[t]), OP.mult, OP.add, "par", "nc%d" % (2 * t))
-        ts(T.nc[:, 2 * t + 1:2 * t + 2], T.par[:], float(-FW), float(FW + REM[t]), OP.mult, OP.add, "par",
-           "nc%d" % (2 * t + 1))
-    for h, nm in ((1, "Ev"), (0, "Od")):
-        cp(T[nm][:], T.D160[:], "D160", nm)
-        for b in range(10):
-            if b % 2 != h:
-                fill(T[nm][:, 16 * b:16 * b + 16], 0.0, nm)
-
-    MAT = {(0, 0): T.Ev[:, 16:144], (0, 1): T.Ev[:, 0:128], (1, 1): T.Od[:, 16:144], (1, 0): T.Od[:, 32:160]}
-
-    def conv(h, l, bank, a=0, e=16):
-        lst, n = [], (e - a) // 2
-        for gp in range(2):
-            i = 0
-            for part in (h, l):
-                for cc in range(2):
-                    lst.append((T[bank][:, n * gp:n * gp + n], MAT[(gp, cc)], T[part][:, a + cc:e:2], i == 0, i == 3))
-                    i += 1
-        return lst
-
-    def codes(t, w):
-        return T.land1[:, 64 * t:64 * t + 32] if w else T.land0[:, 16 * t:16 * t + 16]
-
-    COL = (slice(0, 16), slice(16, 48))
-
-    def arr_s(t, w):
-        act(T.LA[:, COL[w]], codes(t, w), ACT.Copy, "land%d_%d" % (t, w), "LA%d" % w, bias=1184.0)
-        act(T.Lh[:, COL[w]], T.LA[:, COL[w]], ACT.Copy, "LA%d" % w, "Lh%d" % w)
-
-    def arr_u(t, w):
-        ts(T.Lu[:, COL[w]], codes(t, w), float(PAD), None, OP.add, None, "land%d_%d" % (t, w), "Lu%d" % w)
-
-    def arr_l(w):
-        tt(T.Ll[:, COL[w]], T.LA[:, COL[w]], T.Lh[:, COL[w]], OP.subtract, "LA%d Lh%d" % (w, w), "Ll%d" % w)
-        mms(conv("Lh", "Ll", "MS", 16, 48) if w else conv("Lh", "Ll", "MS"), "Lh%d Ll%d Ev Od" % (w, w), "MS")
-
-    def arr_e(w):
-        if not w:
-            act(T.LS[:, 0:16], T.MS[:, 0:16], ACT.Copy, "", "MS LS0")
-        for k in (1, 2) if w else ():
-            for gp in range(2):
-                act(T.LS[:, 16 * k + 8 * gp:16 * k + 8 * gp + 8], T.MS[:, 16 * gp + 8 * k - 8:16 * gp + 8 * k], ACT.Copy,
-                    "", "MS LS%d" % k)
-
-    def masks1(t):
-        act(T.n12[:], T.land1[:, 64 * t + 32:64 * t + 64], ACT.Relu, "land%d_1" % t, "n12", scale=-1.0)
-        act(T.u1[:], T.n12[:, 0:16], ACT.Copy, "n12", "u1", scale=-BIG, bias=BIG)
-
-    def masks2(t):
-        IN, lk = T.land1[:, 64 * t + 48:64 * t + 64], "land%d_1" % t
-        act(T.s21[:], IN, ACT.Relu, lk, "s21")
-        act(T.u2[:], T.s21[:], ACT.Copy, "s21", "u2", scale=BIG)
-        act(T.a2[:], IN, ACT.Abs, lk, "a2")
-        act(T.s20[:], T.a2[:], ACT.Copy, "a2", "s20", scale=-1.0, bias=1.0)
-        for k in (1, 2):
-            act(T.LAk[:, 16 * k - 16:16 * k], kk("LA", k), ACT.Copy, "LA1", "LAk%d" % k, scale=-32.0, bias=32.0 * k)
-
-    def npart(t, k, bs, btok):
-        es = btok == "Es"
-        w0 = 77 * t - REM[t]
-
-        def nu(gp):
-            return lambda: ts(T.nu[:, gp::2], T.nn[:, 8 * gp:8 * gp + 8], T.nc[:, 2 * t + gp:2 * t + gp + 1], None, OP.add,
-                              None, "nn nc%d" % (2 * t + gp), "nu%d" % gp)
-
-        def ctu(ch):
-            return lambda: cp(T.CTu[:, 64 * ch:64 * ch + 64], T.CT[:, ch::4], "CT", "CTu%d" % ch)
-        return [
-            lambda: tt(T.z32[:], kk("LS", k), bs, OP.mult, "LS%d" % k + (" Es" if es else ""), "z32" + ("" if es else " CV")),
-            lambda: ts(T.nn[:], T.z32[:], 5, 1023, OP.arith_shift_right, OP.bitwise_and, "z32", "nn"),
-            nu(0), nu(1),
-            lambda: ts(T.C[:], T.FA[:, w0:2 * FW].indirect(T.nu[:]), float(PAD), None, OP.add, None,
-                       "nu0 nu1 FAx0 FAx1 " + FAtok, "C"),
-            lambda: op("v", lambda e: e.transpose(out=T.CT[:], in_=T.C[:]), "C", "CT"),
-            ctu(3), ctu(0), ctu(1), ctu(2)]
-
-    def xl(k, halves=(slice(0, 16),)):
-        for s in halves:
-            act(T.XL[:, 256 * k + 16 * s.start:256 * k + 16 * s.stop], Xw.indirect(T.Lu[:, 16 * k + s.start:16 * k + s.stop]),
-                ACT.Copy, "X Xpad Lu%d" % min(k, 1), "XL%d_%d" % (k, s.start))
-
-    HALVES = (slice(0, 8), slice(8, 16))
-
-    def qpart(k, off, otok, halves=(slice(0, 16),)):
-        for s in halves:
-            a, e = 16 * s.start, 16 * s.stop
-            tt(T.qq[:, a:e], Xw.indirect(off[:, s]), T.XL[:, 256 * k + a:256 * k + e], OP.max,
-               "X Xpad %s XL%d_%d" % (otok, k, s.start), "qq1" if a else ("qq0" if e < 256 else "qq0 qq1"))
-        for h in range(2):
-            act(T.Q4[:, 512 * h:512 * h + 512], T.qq[:, 128 * h:128 * h + 128].indirect(T.EXu[:]), ACT.Copy,
-                "qq%d EXu" % h, "Q4%d" % h)
-
-    PLACE = {ch: ("DA", T.DA[:, ch:256:4]) for ch in (0, 1, 3)}
-    PLACE[2] = ("DB", T.DB[:, 0:64])
-
-    def starts():
-        mms([(T.DA[:, 0:256], T.I32[:], T.CT[:], True, False),
-             (T.DA[:, 0:256], T.oneb[0:1, :], T.MK[0:1, :], False, False)], "CT I32 oneb MK", "DA")
-        mms([(T.DB[:, 0:64], T.I32[:], T.CT[:, 2::4], True, False),
-             (T.DB[:, 0:64], T.oneb[0:1, :], T.MK2[0:1, :], False, False)], "CT I32 oneb MK2", "DB")
-
-    def sums(ch, ps, last, r):
-        tok, d = PLACE[ch]
-        mms([(d, T.W65[:, 15 - p:143 - p], T["z%d" % ch][:, p::16], False, last and p == ps[-1]) for p in ps], r + " W65", tok)
-
-    def fused(ch, h, w):
-        a, b, q = (0, 64, "Q40 Q41") if h is None else (32 * h, 32 * h + 32, "Q4%d" % h)
-        tt(T["z%d" % ch][:, 16 * a:16 * b], Xw.indirect(T.CTu[:, 64 * ch + a:64 * ch + b]),
-           T.Q4[:, 16 * a:16 * b], OP.subtract, "X Xpad CTu%d %s" % (ch, q), w)
-
-    def absz(a, tok):
-        act(a, a, ACT.Abs, tok, tok)
-
-    ALL = list(range(16))
-
-    def pair(ch, toks):
-        z = T["z%d" % ch]
-        for s in range(2):
-            absz(z[:, s::2], toks[s])
-            sums(ch, ALL[s::2], s == 1 and ch == 1, toks[s])
-
-    def main():
-        for h in range(2):
-            act(T.z3[:, 512 * h:512 * h + 512], Xw.indirect(T.CTu[:, 192 + 32 * h:224 + 32 * h]), ACT.Copy,
-                "X Xpad CTu3", "z3e%d z3o%d" % (h, h))
-        starts()
-        for h in range(2):
-            mms([(T.q4ps[:, 512 * h:512 * h + 512], T.IB[:], T.Q4[:, 512 * h:512 * h + 512], True, True)], "IB Q4%d" % h, "qp%d" % h)
-        fused(0, 0, "z0e z0o")
-        fused(0, 1, "z0e z0o")
-        pair(0, ("z0e", "z0o"))
-        for h in range(2):
-            z, tok = T.z3[:, 512 * h:512 * h + 512], "z3e%d z3o%d" % (h, h)
-            tt(z, z, T.q4ps[:, 512 * h:512 * h + 512], OP.subtract, tok, tok + " qp%d" % h)
-        pair(3, ("z3e0 z3e1", "z3o0 z3o1"))
-        fused(1, None, "z1e z1o")
-        pair(1, ("z1e", "z1o"))
-        fused(2, 0, "z2a")
-        absz(T.z2[:, 0:512], "z2a")
-        fused(2, 1, "z2e z2o")
-        absz(T.z2[:, 512::2], "z2e")
-        sums(2, ALL[0::2], False, "z2a z2e")
-        absz(T.z2[:, 513::2], "z2o")
-        sums(2, ALL[1::2], True, "z2a z2o")
-
-    def scan(b):
-        op("v", lambda e: e.tensor_tensor_scan(out=T["S" + b][:], data0=T["RS" + b][:], data1=T["D" + b][:, 0:256 if b == "A" else 64],
-                                               initial=BIG, op0=OP.max, op1=OP.min), "RS" + b, "S%s D%s" % (b, b))
-
-    MA, MB = T.SA[:, 15::16], T.SB[:, 3::4]
-
-    def chain(k):
-        tt(T.t1[:], T.Mu[:], MB, OP.min, "Mu SB", "t1")
-        tt(T.t2[:], T.t1[:], T["w%d" % k][:], OP.max, "t1 w%d" % k, "t2")
-        ts(T.bi[:], T.t2[:], 4095, None, OP.bitwise_and, None, "t2", "bi")
-        cp(T.bh[:], T.bi[:], "bi", "bh")
-        cp(T.bu[:], T.bi[:], "bi", "bu")
-        tt(T.bl[:], T.bi[:], T.bh[:], OP.subtract, "bi bh", "bl")
-        mms(conv("bh", "bl", "CV"), "bh bl Ev Od", "CV")
-        qpart(k, T.bu, "bu")
-
-    def keys(k):
-        tc = T.Tk[:, k:k + 1]
-        r = [lambda: tt(kk("K", k), MA, MB, OP.min, "SA SB", "K%d" % k),
-             lambda: ts(kk("B", k), kk("K", k), 4095, None, OP.bitwise_and, None, "K%d" % k, "B%d" % k)]
-        if k == 0:
-            r.append(lambda: ts(kk("lv", 0), kk("K", 0), tc, None, OP.is_lt, None, "K0 Tk", "lv0"))
-        else:
-            r.append(lambda: ts(T.lt[:], kk("K", k), tc, None, OP.is_lt, None, "K%d Tk" % k, "lt"))
-            r.append(lambda: tt(kk("lv", k), T.lt[:], T["g%d" % k][:], OP.mult, "lt g%d" % k, "lv%d" % k))
-        r.append(lambda: tt(T.yo[:], kk("B", k), kk("lv", k), OP.mult, "B%d lv%d" % (k, k), "yo"))
-        r.append(lambda: cp(kk("yu", k), T.yo[:], "yo", "yu%d" % k))
-        return r
-
-    def send(t, w, src, dst_ap):
-        dst = T.cores[(rank + 1) % n_ranks if t < NV - 1 else (rank - t) % n_ranks]
-        before("g", ["src%d_%d" % (t, w)], [])
-        rid, pid = topo.addr(dst, core)
-        ar = "ar%d_%d" % (t + 1, w)
-        g.remote_dma(dst_ap, src, T.sem[ar], T.sem.ls, pid, rid, topo.mask(core, dst))
-        ne = len(topo.engines(core, dst))
-        sent[0] += ne
-        lastw["land%d_%d" % (t + 1, w)] = (ar, ne, "remote")
-
-    def rewire0_pre(t):
-        tt(T.rz0[:], kk("LA", 0), T.Er[:], OP.mult, "LA0 Er", "rz0")
-        ts(T.NW0[:], T.rz0[:], 5, 2047, OP.arith_shift_right, OP.bitwise_and, "rz0", "NW0")
-        tt(T.df0[:], T.NW0[:], T.land0[:, 16 * t:16 * t + 16], OP.subtract, "NW0 land%d_0" % t, "df0")
-
-    def rewire0(t):
-        tt(T.x0[:], T.df0[:], kk("lv", 0), OP.mult, "df0 lv0", "x0")
-        src = T.src0[:, 16 * t:16 * t + 16]
-        tt(src, T.NW0[:], T.x0[:], OP.subtract, "NW0 x0", "src%d_0" % t)
-        send(t, 0, src, T.land0[:, 16 * t + 16:16 * t + 32])
-
-    def rewire1_p1():
-        return [lambda: tt(T.px[:], kk("B", 0), T.Ep[:], OP.subtract, "B0 Ep", "px"),
-                lambda: tt(T.px[:], T.px[:], kk("lv", 0), OP.mult, "px lv0", "px"),
-                lambda: ts(T.NW[:, 32:48], kk("lv", 0), -1.0, None, OP.add, None, "lv0", "NWp1"),
-                lambda: tt(T.P12[:, 0:16], T.px[:], T.Ep[:], OP.add, "px Ep", "P1")]
-
-    def rewire1_pre(t):
-        return [lambda: tt(T.qx[:], kk("B", 1), T.P12[:, 0:16], OP.subtract, "B1 P1", "qx"),
-                lambda: tt(T.qx[:], T.qx[:], kk("lv", 1), OP.mult, "qx lv1", "qx"),
-                lambda: tt(T.P12[:, 16:32], T.qx[:], T.P12[:, 0:16], OP.add, "qx P1", "P2"),
-                lambda: tt(T.NW[:, 48:64], T.pa[:], T.pb[:], OP.max, "pa pb", "NWp2"),
-                lambda: tt(T.rz12[:], T.LA[:, 16:48], T.P12[:], OP.mult, "LA1 P1 P2", "rz12"),
-                lambda: tt(T.rk12[:], T.rz12[:], T.LAk[:], OP.add, "rz12 LAk1 LAk2", "rk12"),
-                lambda: ts(T.NW[:, 0:32], T.rk12[:], 5, 2047, OP.arith_shift_right, OP.bitwise_and, "rk12", "NWl"),
-                lambda: tt(T.df[:], T.NW[:], T.land1[:, 64 * t:64 * t + 64], OP.subtract, "NWl NWp1 NWp2 land%d_1" % t, "df")]
-
-    def rewire1(t):
-        src = T.src1[:, 64 * t:64 * t + 64]
-        return [lambda: tt(T.xx[:], T.df[:], T.lvd[:], OP.mult, "df lvd0 lvd1", "xx"),
-                lambda: tt(src, T.NW[:], T.xx[:], OP.subtract, "NWl NWp1 NWp2 xx", "src%d_1" % t),
-                lambda: send(t, 1, src, T.land1[:, 64 * t + 64:64 * t + 128])]
-
-    def thresholds():
-        return [lambda: op("v", lambda e: e.tensor_reduce(out=T.cnt[:], in_=T.CV[:, 0:48], axis=AxisListType.X, op=OP.add), "", "cnt CV"),
-                lambda: ts(T.ai[:], T.cnt[:], -1.0, 6144.0, OP.mult, OP.add, "cnt", "ai"),
-                lambda: ts(T.ai2[:], T.ai[:], 31, None, OP.bitwise_and, None, "ai", "ai2"),
-                lambda: ts(T.af[:], T.ai2[:], 65536.0, None, OP.mult, None, "ai2", "af"),
-                lambda: ts(T.Tk[:], T.thk[:], T.af[:], None, OP.add, None, "thk af", "Tk")]
-
-    ts(T.Ep[:], T.exi[:], float(PAD), None, OP.add, None, "exi", "Ep")
-    cp(T.eh[:], T.Ep[:], "Ep", "eh")
-    tt(T.el[:], T.Ep[:], T.eh[:], OP.subtract, "Ep eh", "el")
-    mms(conv("eh", "el", "CV"), "eh el Ev Od", "CV")
-    act(T.Es[:], T.CV[:, 0:16], ACT.Copy, "", "CV Es")
-    cp(T.land0[:, 0:16], T.lci[:, 0:16], "lci", "land0_0")
-    cp(T.Eu[:], T.Ep[:], "Ep", "Eu")
-    arr_s(0, 0)
-    arr_u(0, 0)
-    arr_l(0)
-    arr_e(0)
-    xl(0, HALVES)
-    cp(T.Er[:], T.exi[:], "exi", "Er")
-    ts(T.W65[:], T.W[:], 65536.0, None, OP.mult, None, "W", "W65")
-    cp(T.IB[:], T.I32[:], "I32", "IB")
-    ts(T.RSA[:], T.RSA[:], BIG, None, OP.mult, None, "RSA", "RSA")
-    ts(T.RSB[:], T.RSB[:], BIG, None, OP.mult, None, "RSB", "RSB")
-    fill(T.MK[0:1, 2::4], BIG, "MK")
-    np_ = npart(0, 0, T.Es[:], "Es")
-    weave(np_[0:4], [])
-    qpart(0, T.Eu, "Eu", HALVES)
-    cp(T.land1[:, 0:32], T.lci[:, 16:48], "lci", "land0_1")
-    ts(T.tsel[:], T.tsel[:], 65536.0, None, OP.mult, None, "tsel", "tsel")
+    ts(T.RS[:], T.pm[:], 0.0, BIG, OP.is_equal, OP.mult, "pm", "RS", cyc(128))
+    ts(T.RS[:], T.RS[:], -LOW, None, OP.add, None, "RS", "RS", cyc(128))
+    ts(T.pm[:], T.pm[:], T.p15f[:], None, OP.is_equal, None, "pm p15f", "pm", cyc(128))
+    cp(T.e15u[:], T.e15[:], "e15", "e15u")
+    cp(T.e1u[:], T.e1[:], "e1", "e1u")
     ts(T.base[:], T.b128[:], T.p8[:], None, OP.add, None, "b128 p8", "base")
-    fill(T.mone[:], -1.0, "mone")
-    dma("y", T.yi[:, 0:16], T.mone[:], "dout", 64, "mone", "yi0")
-    weave(np_[4:], [])
-    cp(T.land1[:, 32:64], T.upi[:, 16:48], "upi", "land0_1")
     cp(T.thf[:], T.thi[:], "thi", "thf")
     cp(T.wtf[:], T.wti[:], "wti", "wtf")
-    ts(T.SW[:], T.W[:], T.wtf[:], None, OP.mult, None, "W wtf", "SW")
-    for b in range(2):
-        dma("y", T.FA[:, b * FW + 1024:(b + 1) * FW], T.FA[:, b * FW:b * FW + FW - 1024], "dfw", 32, FAtok, "FAx%d" % b)
+    act(T.SW[:], T.W[:], ACT.Copy, "W wtf", "SW", scale=T.wtf[:])
+    mms([(T.MS[:, 0:3], T.tsel[:], T.thf[:], True, True)], "tsel thf", "MS", 256)
+    act(T.thk[:], T.MS[:, 0:3], ACT.Copy, "", "MS thk", scale=65536.0)
+    act(T.Tk[:], T.thk[:], ACT.Copy, "thk", "Tk")
+    dma("y", T.yi[:, 0:16], T.mone[:], "do0", 16, "mone", "out0")
 
+    ts(T.Ep[:], T.exi[:], float(PAD), None, OP.add, None, "exi", "Ep")
+    ts(T.Eu[:], T.exi[:], float(PAD), None, OP.add, None, "exi", "Eu")
+    act(T.nEp[:], T.Ep[:], ACT.Copy, "Ep", "nEp", scale=-1.0)
+    cp(T.land[:, 0:16], T.lci[:, 0:16], "lci", "land0A")
+    cp(T.land[:, 32:64], T.lci[:, 16:48], "lci", "land0B land0C")
+    cp(T.land[:, 16:32], T.upi[:, 16:32], "upi", "land0B")
+    cp(T.land[:, 64:80], T.upi[:, 32:48], "upi", "land0C")
+
+    MAT = {(0, 0): T.Ev[:, 16:144], (0, 1): T.Ev[:, 0:128], (1, 1): T.Od[:, 16:144], (1, 0): T.Od[:, 32:160]}
+    REM = [(77 * t) % 8 for t in range(NV)]
+    MSG = {"A": (0, 16), "B": (16, 48), "C": (48, 80)}
+
+    def land(t, a, b):
+        return T.land[:, 80 * t + a:80 * t + b]
+
+    def arrive(t, k):
+        a = (0, 32, 48)[k]
+        codes, tok = land(t, a, a + 16), "land%d%s" % (t, "ABC"[k])
+        act(col("LA", k), codes, ACT.Copy, tok, "LA%d" % k, bias=1184.0)
+        ts(col("Lu", k), codes, float(PAD), None, OP.add, None, tok, "Lu%d" % k)
+
+    def masks(t):
+        I1, I2, tok = land(t, 16, 32), land(t, 64, 80), "land%dB" % t
+        act(T.u1[:], I1, ACT.Relu, tok + " c4k", "u1", scale=4096.0, bias=T.c4k[:])
+        tt(T.w1[:], I1, T.nEp[:], OP.mult, tok + " nEp", "w1")
+        tok = "land%dC" % t
+        act(T.u2[:], I2, ACT.Relu, tok, "u2", scale=4096.0)
+        act(T.s2[:, 16:32], I2, ACT.Relu, tok, "s21")
+        act(T.n2[:], I2, ACT.Relu, tok, "n2", scale=-1.0)
+        act(T.a2[:], I2, ACT.Abs, tok, "a2")
+        act(T.s2[:, 0:16], T.a2[:], ACT.Copy, "a2", "s20", scale=-1.0, bias=1.0)
+        tt(T.nE[:], T.n2[:], T.Ep[:], OP.mult, "n2 Ep", "nE")
+
+    def facts(t, k, h, b, btok):
+        a, e = (0, 16) if h is None else (8 * h, 8 * h + 8)
+        n, w0 = e - a, 77 * t - REM[t]
+        tt(T.z32[:, a:e], col("LA", k, h), b, OP.mult, toks(btok + " LA%d" % k, h), toks("z32%", h))
+        ts(T.nn[:, a:e], T.z32[:, a:e], 5, 1023, OP.arith_shift_right, OP.bitwise_and, toks("z32%", h), toks("nn%", h))
+        ts(T.nu[:, a:e], T.nn[:, a:e], float(REM[t]), None, OP.add, None, toks("nn%", h), toks("nu%", h))
+        cp(T.C[:, 16 * a:16 * e], T.FA[:, w0:FW].indirect(T.nu[:, a:e]), toks("nu% FAx FA1 FA2", h), toks("C%", h), gat(16 * n))
+        op("v", lambda v: v.transpose(out=T.CT[:, 16 * a:16 * e], in_=T.C[:, 16 * a:16 * e]), toks("C%", h), toks("CT%", h), cyc(8 * n))
+
+    def lists(h):
+        mms([(T.PB[:, 0:128], T.oneb[32:33, :], T.MK[32:33, 0:128], True, False)], "oneb MK", "PB", 128)
+        mms([(T.PB[:, c:128:8], MAT[(c % 2, x)], T.CT[:, 128 * h + 32 * (c // 2) + 16 * x:128 * h + 32 * (c // 2) + 16 * x + 16],
+              False, c == 7 and x == 1) for c in range(8) for x in range(2)], "CT%d Ev Od" % h, "PB")
+        cp(T.CTu[:, 128 * h:128 * h + 128], T.PB[:, 0:128], "", "PB CTu%d" % h, cyc(128))
+        KB = T["KB%d" % h][:, 0:128]
+        mms([(KB, T.oneb[0:65, :], T.MK[0:65, 0:128], True, False), (KB, T.C[:, 128 * h:128 * h + 128], T.I16[:], False, False)],
+            "oneb MK I16 C%d" % h, "KB%d" % h, 128)
+
+    def xl(k, h=None):
+        a, e = (0, 16) if h is None else (8 * h, 8 * h + 8)
+        o, i, r = T.XL[:, 256 * k + 16 * a:256 * k + 16 * e], Xw.indirect(col("Lu", k, h)), XT + " Lu%d" % k
+        if h == 0:
+            cp(o, i, r, "XL%d_0" % k, gat(128))
+        else:
+            act(o, i, ACT.Copy, r, toks("XL" + str(k) + "_%", h), gat(16 * (e - a)))
+
+    def qtok(h, n):
+        return " ".join("Q%d_%d" % (h, i) for i in (1, 2, 4) if i < 2 * n)
+
+    def qpart(k, h, off, otok):
+        Q = T["Q%d" % h]
+        tt(Q[:, 0:128], Xw.indirect(off), T.XL[:, 256 * k + 128 * h:256 * k + 128 * h + 128], OP.max,
+           "%s %s XL%d_%d" % (XT, otok, k, h), "Q%d_1" % h, gat(128))
+        for n in (1, 2):
+            cp(Q[:, 128 * n:256 * n], Q[:, 0:128 * n], qtok(h, n), "Q%d_%d" % (h, 2 * n), cyc(64 * n))
+
+    bank = [0]
+
+    def main(h):
+        Z, Y, Q, kb = T["Z%d" % h], T["Y%d" % h], T["Q%d" % h], "KB%d" % h
+        for (who, a, e) in CHUNKS:
+            n, z, tok = e - a, Z[:, 128 * a:128 * e], "Z%d_%d" % (h, a)
+            lst, sums = Xw.indirect(T.CTu[:, 128 * h + 8 * a:128 * h + 8 * e]), [(Z, T.W1)]
+            if who != "D":
+                tt(z, lst, Q[:, 0:128 * n], OP.subtract, "%s CTu%d %s" % (XT, h, qtok(h, n)), tok, gat(128 * n))
+            if who == "A":
+                sums, src = [(Y, T.W2), (Z, T.W1)], tok
+                for u in range(a, e, 2):
+                    v = min(u + 2, e)
+                    tok += " Y%d_%d" % (h, u)
+                    ts(Y[:, 128 * u:128 * v], Z[:, 128 * u:128 * v], 0.0, None, OP.min, None, src, "Y%d_%d" % (h, u), cyc(64 * (v - u)))
+            elif who == "B":
+                act(z, z, ACT.Abs, tok, tok, cyc(128 * n))
+            else:
+                d = "D%d" % bank[0]
+                bank[0] = (bank[0] + 1) % 3
+                act(z, lst, ACT.Copy, "%s CTu%d" % (XT, h), tok, gat(128 * n))
+                mms([(T[d][:, 0:128 * n], T.NI[:], Q[:, 0:128 * n], True, False)], "NI " + qtok(h, n), d, 128 * n)
+                mms([(T[d][:, 0:128 * n], T.IB[:], z, False, True)], "IB " + tok, d, 128 * n)
+                act(z, T[d][:, 0:128 * n], ACT.Abs, "", d + " " + tok, cyc(128 * n))
+            mms([(T[kb][:, m:128:16], src[:, 128 * m:128 * m + 128], w[:], False, m == 15 and src is Z)
+                 for m in range(a, e) for (src, w) in sums], tok + " W1 W2", kb)
+
+    def least(k, h):
+        SA = T["SA%d" % h]
+        op("v", lambda e: e.tensor_tensor_scan(out=SA[:], data0=T.RS[:], data1=T["KB%d" % h][:, 0:128], initial=BIG,
+                                               op0=OP.max, op1=OP.min), "RS", "KB%d SA%d" % (h, h), cyc(128))
+        tt(T.KX[:], SA[:, 0:128].indirect(T.e15u[:, 0:8]), T.pm[:], OP.mult, "SA%d e15u pm" % h, "KX", gat(128))
+        mms([(T.KN[:, 0:8], T.KX[:], T.W[:], True, True)], "KX W", "KN", 256)
+        if k == 0:
+            ts(col("K", 0, h), T.KN[:, 0:8], LOW, T.Tk[:, 0:1], OP.add, OP.min, "Tk", "KN K0_%d" % h)
+        else:
+            tt(col("K", k, h), T.KN[:, 0:8], col("Tg%d" % k, 0, h), OP.min, "Tg%d" % k, "KN K%d_%d" % (k, h))
+        ts(col("B", k, h), col("K", k, h), 4095, None, OP.bitwise_and, None, "K%d_%d" % (k, h), "B%d_%d" % (k, h))
+
+    def follow(t, k, h):
+        least(k - 1, h)
+        tt(col("t1", 0, h), col("B", k - 1, h), col("u%d" % k, 0, h), OP.min, "B%d_%d u%d" % (k - 1, h, k), "t1%d" % h)
+        tt(col("bi", 0, h), col("t1", 0, h), col("w%d" % k, 0, h), OP.max, "t1%d w%d" % (h, k), "bi%d" % h)
+        facts(t, k, h, col("bi", 0, h), "bi%")
+        cp(col("bu", 0, h), col("bi", 0, h), "bi%d" % h, "bu%d" % h)
+        qpart(k, h, col("bu", 0, h), "bu%d" % h)
+        lists(h)
+
+    def lvc(k, h=None):
+        return col("lv", (0, 1, 3)[k], h)
+
+    def send(t, m, r):
+        a, b = MSG[m]
+        tt(T.xx[:, a:b], T.df[:, a:b], T.lv[:, a:b], OP.mult, ("dfA " if m == "A" else "dfB ") + r, "xx" + m, cyc(2 * (b - a)))
+        src, tok = T.src[:, 80 * t + a:80 * t + b], "src%d%s" % (t, m)
+        tt(src, T.NW[:, a:b], T.xx[:, a:b], OP.subtract, ("NW0" if m == "A" else "NWl NW1 NW2") + " xx" + m, tok, cyc(2 * (b - a)))
+        dst = T.cores[(rank + 1) % n_ranks if t < NV - 1 else (rank - t) % n_ranks]
+        w = ["land%d%s" % (t + 1, m)]
+
+        def issue():
+            before("g", [tok], [])
+            rid, pid = topo.addr(dst, core)
+            ar = "ar%d%s" % (t + 1, m)
+            g.remote_dma(land(t + 1, a, b), src, T.sem[ar], T.sem.ls, pid, rid, topo.mask(core, dst))
+            ne = len(topo.engines(core, dst))
+            sent[0] += ne
+            lastw[w[0]] = (ar, ne, "remote")
+        jobs.append(("g", issue, [tok], w, 0.4, FAR if t or m != "A" else FAR + 3.0, lazy[0]))
+
+    def after0(t):
+        ts(lvc(0), col("B", 0), 0.0, None, OP.is_gt, None, "B0_0 B0_1", "lv0")
+        tt(T.g1[:], lvc(0), land(t, 16, 32), OP.is_gt, "lv0 land%dB" % t, "g1")
+        act(T.Tg1[:], T.g1[:], ACT.Copy, "g1 Tk", "Tg1", scale=T.Tk[:, 1:2], bias=-LOW)
+        tt(T.sB[:], T.s2[:, 0:16], col("B", 0), OP.mult, "s20 B0_0 B0_1", "sB")
+        tt(T.w2[:], T.sB[:], T.nE[:], OP.add, "sB nE", "w2")
+        tt(T.rz0[:], col("LA", 0), T.exi[:], OP.mult, "LA0 exi", "rz0")
+        ts(T.NW[:, 0:16], T.rz0[:], 5, 2047, OP.arith_shift_right, OP.bitwise_and, "rz0", "NW0")
+        tt(T.df[:, 0:16], T.NW[:, 0:16], land(t, 0, 16), OP.subtract, "NW0 land%dA" % t, "dfA")
+        send(t, "A", "lv0")
+
+    def after1(t):
+        ts(lvc(1), col("B", 1), 0.0, None, OP.is_gt, None, "B1_0 B1_1", "lv1")
+        act(T.dd[:], T.lv[:, 0:32], ACT.Copy, "lv0 lv1", "dd", scale=-1.0, bias=1.0)
+        tt(T.sd[:], T.s2[:], T.dd[:], OP.mult, "s20 s21 dd", "sd")
+        tt(T.g2[:], T.sd[:, 0:16], T.sd[:, 16:32], OP.is_equal, "sd", "g2")
+        act(T.Tg2[:], T.g2[:], ACT.Copy, "g2 Tk", "Tg2", scale=T.Tk[:, 2:3], bias=-LOW)
+        cp(T.yu[:, 0:32], T.B[:, 0:32], "B0_0 B0_1 B1_0 B1_1", "yu01")
+        act(T.y0[:], Xw.indirect(col("yu", 0)), ACT.Copy, XT + " yu01", "y0", gat(256))
+        for h in range(2):
+            s = slice(128 * h, 128 * h + 128)
+            tt(T.y01[:, s], Xw.indirect(col("yu", 1, h)), T.y0[:, s], OP.max, XT + " yu01 y0", "y01%d" % h, gat(128))
+        for k in (1, 2):
+            tt(T.px[:], col("dd", k - 1), T.Ep[:] if k == 1 else col("P", 0), OP.mult, "dd " + ("Ep", "P1")[k - 1], "px")
+            tt(col("P", k - 1), T.px[:], col("B", k - 1), OP.add, "px B%d_0 B%d_1" % (k - 1, k - 1), "P%d" % k)
+        act(T.Pu[:], T.P[:], ACT.Copy, "P1 P2", "Pu", bias=-float(PAD))
+        tt(T.rz[:], T.LA[:, 16:48], T.Pu[:], OP.mult, "LA1 LA2 Pu", "rz")
+        tt(T.rk[:], T.rz[:], T.K32[:], OP.add, "rz K32", "rk")
+        ts(T.NW[:, 32:64], T.rk[:], 5, 2047, OP.arith_shift_right, OP.bitwise_and, "rk", "NWl")
+        ts(T.NW[:, 16:32], lvc(0), -1.0, None, OP.add, None, "lv0", "NW1")
+        act(T.pa[:], lvc(1), ACT.Copy, "lv1", "pa", scale=2.0, bias=-1.0)
+        tt(T.NW[:, 64:80], T.NW[:, 16:32], T.pa[:], OP.max, "NW1 pa", "NW2")
+        tt(T.df[:, 16:80], T.NW[:, 16:80], land(t, 16, 80), OP.subtract, "NWl NW1 NW2 land%dB land%dC" % (t, t), "dfB", cyc(128))
+        act(T.lv[:, 32:48], lvc(1), ACT.Copy, "lv1", "lv1d")
+        send(t, "B", "lv1 lv1d")
+
+    def write(t, h):
+        s = slice(8 * h, 8 * h + 8)
+        least(2, h)
+        cp(col("yu", 2, h), col("B", 2, h), "B2_%d" % h, "yu2_%d" % h)
+        y = T.yy[:, 128 * h:128 * h + 128]
+        tt(y, Xw.indirect(col("yu", 2, h)), T.y01[:, 128 * h:128 * h + 128], OP.max, XT + " yu2_%d y01%d" % (h, h), "yy%d" % h, gat(128))
+        mms([(T.MS[:, 0:8], y, T.SW[:], True, True)], "SW yy%d" % h, "MS")
+        cp(T.si[:, s], T.MS[:, 0:8], "", "MS si%d" % h)
+        ts(T.sm[:, s], T.si[:, s], 7, None, OP.bitwise_and, None, "si%d" % h, "sm%d" % h)
+        tt(T.SX[:], T.sm[:, s].indirect(T.e1u[:, 0:8]), T.pm[:], OP.mult, "sm%d e1u pm" % h, "SX", gat(128))
+        mms([(T.MS[:, 0:8], T.I16[:], T.base[:, s], True, False)], "I16 base", "MS")
+        mms([(T.MS[:, 0:8], T.SX[:], T.Wb[:], False, True)], "SX Wb", "MS")
+        cp(T.wu[:, s], T.MS[:, 0:8], "", "MS wu%d" % h)
+
+    def scatter(t, h):
+        M = PAD + 1024
+        win = T.X[:, M:M + 1024] if h else T.X[:, 0:M]
+        op("v", lambda e: e.tensor_copy(out=win.indirect(T.wu[:, 8 * h:8 * h + 8]), in_=T.yy[:, 128 * h:128 * h + 128]),
+           "wu%d yy%d" % (h, h), "X1" if h else "X0 Xpad", 0.06 + 128 * SCATTER * CYC)
+        if t == NV - 1:
+            dma("sy"[h], T.yx[:, 1024 * h:1024 * h + 1024], T.X[:, PAD + 1024 * h:M + 1024 * h], "dy%d" % h, 16, "X%d" % h, "yx%d" % h, 3.0)
+
+    def thresholds():
+        mms([(T.MS[:, 0:32], T.oneb[:], T.lv[:, 0:32], True, True), (T.MS[:, 32:48], T.oneb[:], lvc(2), True, True)],
+            "oneb lv0 lv1 lv2_48", "MS")
+        op("s", lambda e: e.activation(out=T.cdum[:], in_=T.MS[:, 0:48], func=ACT.Copy, bias=128.0, scale=-1.0,
+                                       accum_out=T.cnt[:]), "", "MS cdum cnt", cyc(90))
+        cp(T.ai[:], T.cnt[:], "cnt", "ai")
+        ts(T.ai2[:], T.ai[:], 31, None, OP.bitwise_and, None, "ai", "ai2")
+        ts(T.af[:], T.ai2[:], 65536.0, None, OP.mult, None, "ai2", "af")
+        act(T.Tk[:], T.thk[:], ACT.Identity, "thk af", "Tk", bias=T.af[:])
+
+    def aside(*calls):
+        lazy[0] = True
+        for c in calls:
+            c[0](*c[1:])
+        lazy[0] = False
+
+    arrive(0, 0)
+    facts(0, 0, None, T.Ep[:], "Ep")
+    dma("y", T.FA[:, 1024:FW], T.FA[:, 0:FW - 1024], "dfw", 16, "FA1 FA2", "FAx")
+    lazy[0] = False
     for t in range(NV):
         more = t < NV - 1
-        main()
-        if t == 0:
-            mms([(T.MS[:, 0:3], T.tsel[:], T.thf[:], True, True)], "tsel thf", "MS")
-            act(T.thk[:], T.MS[:, 0:3], ACT.Copy, "", "MS thk")
-            act(T.Tk[:], T.thk[:], ACT.Copy, "thk", "Tk")
-        arr_u(t, 1)
-        arr_s(t, 1)
-        masks1(t)
-        xl(1)
-        rewire0_pre(t)
-        scan("A")
-        arr_l(1)
-        masks2(t)
-        arr_e(1)
-        tt(T.w1[:], T.n12[:, 0:16], T.Ep[:], OP.mult, "n12 Ep", "w1")
-        tt(T.Mu[:], MA, T.u1[:], OP.min, "SA u1", "Mu")
-        tt(T.nE[:], T.n12[:, 16:32], T.Ep[:], OP.mult, "n12 Ep", "nE")
-        scan("B")
-        chain(1)
-        ks = keys(0)
-        weave(ks[0:2], [])
-        weave(npart(t, 1, T.CV[:, 0:16], "CV"), ks[2:])
-        main()
-        xl(2)
-        act(T.y0[:], Xw.indirect(kk("yu", 0)), ACT.Copy, "X Xpad yu0", "y0")
-        rewire0(t)
-        tt(T.sB[:], T.s20[:], kk("B", 0), OP.mult, "s20 B0", "sB")
-        scan("A")
-        weave([lambda: tt(T.w2[:], T.sB[:], T.nE[:], OP.add, "sB nE", "w2"),
-               lambda: tt(T.Mu[:], MA, T.u2[:], OP.min, "SA u2", "Mu"),
-               lambda: tt(T.g1[:], T.n12[:, 0:16], kk("lv", 0), OP.max, "n12 lv0", "g1"),
-               lambda: tt(T.ga[:], T.s20[:], kk("lv", 0), OP.mult, "s20 lv0", "ga")], rewire1_p1())
-        scan("B")
-        chain(2)
-        ks = keys(1)
-        weave(ks[0:2], [])
-        weave(npart(t, 2, T.CV[:, 0:16], "CV"), ks[2:])
-        main()
-        if more:
-            arr_u(t + 1, 0)
-            arr_s(t + 1, 0)
-        act(T.pb[:], kk("lv", 0), ACT.Copy, "lv0", "pb", bias=-1.0)
-        act(T.pa[:], kk("lv", 1), ACT.Copy, "lv1", "pa", scale=2.0, bias=-1.0)
-        tt(T.gb[:], T.s21[:], kk("lv", 1), OP.mult, "s21 lv1", "gb")
-        tt(T.ga[:], T.ga[:], T.n12[:, 16:32], OP.max, "ga n12", "ga")
-        tt(T.y01[:], Xw.indirect(kk("yu", 1)), T.y0[:], OP.max, "X Xpad yu1 y0", "y01")
-        scan("A")
-        weave([lambda: tt(T.g2[:], T.ga[:], T.gb[:], OP.max, "ga gb", "g2"),
-               (lambda: (arr_l(0), arr_e(0))) if more else None], rewire1_pre(t))
-        scan("B")
-        np_ = npart(t + 1, 0, T.Es[:], "Es") if more else []
-        weave(keys(2), [None] * 3 + np_[0:4])
         for h in range(2):
-            act(T.lvd[:, 32 * h:32 * h + 32], T.lv[:, 16:48], ACT.Copy, "lv1 lv2", "lvd%d" % h)
-        tt(T.yy[:], Xw.indirect(kk("yu", 2)), T.y01[:], OP.max, "X Xpad yu2 y01", "yy")
-        mms([(T.CV[:, 0:16], T.SW[:, 15 - p:143 - p], T.yy[:, p::16], p == 0, p == 15) for p in ALL], "SW yy", "CV")
-        weave(np_[4:], [])
-        put = [lambda: cp(T.si[:], T.CV[:, 0:16], "", "si CV"),
-               lambda: ts(T.sm[:], T.si[:], 7, None, OP.bitwise_and, None, "si", "sm"),
-               lambda: tt(T.sa[:], T.sm[:], T.base[:], OP.add, "sm base", "sa")]
+            lists(h)
+            xl(0, h)
+            qpart(0, h, col("Eu", 0, h), "Eu")
+        aside((arrive, t, 1), (arrive, t, 2), (masks, t), (xl, 1), (xl, 2))
+        main(0)
+        main(1)
+        follow(t, 1, 0)
+        main(0)
+        follow(t, 1, 1)
+        aside((after0, t))
+        main(1)
+        follow(t, 2, 0)
+        main(0)
+        follow(t, 2, 1)
+        aside((after1, t))
         if more:
-            put.append(lambda: cp(T.wu[:], T.sa[:], "sa", "wu"))
-            weave(put, rewire1(t))
-            op("v", lambda e: e.tensor_copy(out=Xw.indirect(T.wu[:]), in_=T.yy[:]), "wu yy", "X Xpad")
-            xl(0, HALVES)
-            mms([(T.CV[:, 0:48], T.oneb[:], T.lv[:], True, True)], "oneb lv0 lv1 lv2", "CV")
-            th = thresholds()
-            weave(th[0:3], [])
-            qpart(0, T.Eu, "Eu", HALVES)
-            weave(th[3:], [])
-        else:
-            weave(rewire1(t), put)
-            M = PAD + 1024
-            cp(T.wu[:, 0:8], T.sa[:, 0:8], "sa", "wu0")
-            ts(T.wu[:, 8:16], T.sa[:, 8:16], float(-M), None, OP.add, None, "sa", "wu1")
-            op("v", lambda e: e.tensor_copy(out=T.X[:, 0:M].indirect(T.wu[:, 0:8]), in_=T.yy[:, 0:128]), "wu0 yy X", "Xpad")
-            op("v", lambda e: e.tensor_copy(out=T.X[:, M:M + 1024].indirect(T.wu[:, 8:16]), in_=T.yy[:, 128:256]), "wu1 yy", "X")
-            dma("s", T.yx[:, 0:1024], T.X[:, PAD:M], "dy", 32, "Xpad", "yxo0")
-            dma("s", T.yx[:, 1024:2048], T.X[:, M:M + 1024], "dy", 32, "X", "yxo1")
+            aside((arrive, t + 1, 0), (facts, t + 1, 0, None, T.Ep[:], "Ep"))
+        main(1)
+        write(t, 0)
+        write(t, 1)
+        scatter(t, 0)
+        scatter(t, 1)
+        for a in (48, 64):
+            ts(T.lv[:, a:a + 16], col("B", 2), 0.0, None, OP.is_gt, None, "B2_0 B2_1", "lv2_%d" % a)
+        send(t, "C", "lv2_48 lv2_64")
+        if more:
+            aside((thresholds,))
 
-    dma("y", T.yl[:, 0:16], T.land0[:, 16 * NV:16 * NV + 16], "dout", 64, "land%d_0" % NV, "ylo0")
-    dma("y", T.yl[:, 16:48], T.land1[:, 64 * NV:64 * NV + 32], "dout", 64, "land%d_1" % NV, "ylo1")
-    dma("y", T.yi[:, 16:48], T.land1[:, 64 * NV + 32:64 * NV + 64], "dout", 64, "land%d_1" % NV, "yio1")
-    need("g", "dout", 64)
-    need("g", "dy", 32)
+    dma("y", T.yl[:, 0:16], land(NV, 0, 16), "do1", 16, "land%dA" % NV, "out1")
+    dma("y", T.yl[:, 16:32], land(NV, 32, 48), "do2", 16, "land%dB" % NV, "out2")
+    dma("y", T.yi[:, 16:32], land(NV, 16, 32), "do3", 16, "land%dB" % NV, "out3")
+    dma("y", T.yl[:, 32:48], land(NV, 48, 64), "do4", 16, "land%dC" % NV, "out4")
+    dma("s", T.yi[:, 32:48], land(NV, 64, 80), "do5", 16, "land%dC" % NV, "out5")
+
+    if not ORDER:
+        ORDER.extend(issue_order(jobs))
+    for i in ORDER:
+        jobs[i][1]()
+    for sem in ["do%d" % i for i in range(6)] + ["dy0", "dy1"]:
+        need("g", sem, 16)
     need("g", "ls", sent[0])
     for q in ("v", "s", "p", "g"):
         need("g", "c" + q, count[q])

@@ -4,8 +4,10 @@ OP = AluOpType
 ACT = ActivationFunctionType
 NV, NR, PAD, FW = 4, 3, 32, 1264
 ROT = 864
-CHUNKS = [("A", 0, 4), ("D", 4, 8), ("A", 8, 10), ("D", 10, 13), ("D", 13, 16)]
-QREP, BIG = 4, 2.0 ** 25
+SIX = [("A", 0, 3), ("D", 3, 7), ("D", 7, 10), ("D", 10, 13), ("A", 13, 16)]
+FIVE = [("A", 0, 2), ("D", 2, 6), ("D", 6, 10), ("D", 10, 13), ("A", 13, 16)]
+CHUNKS = [[SIX, SIX], [FIVE, FIVE], [FIVE, SIX]]
+BIG = 2.0 ** 25
 LOW = 240 * 65536.0
 
 SCRATCH = {}
@@ -20,7 +22,7 @@ _decl("sbuf", "bfloat16", "X", 2080)
 _decl("sbuf", "int32", "FA", FW)
 _decl("sbuf", "float16", "C CT", 256)
 _decl("sbuf", "uint16", "CTu", 256)
-_decl("sbuf", "bfloat16", "Q0 Q1", 128 * QREP)
+_decl("sbuf", "bfloat16", "Q0 Q1", 384)
 _decl("sbuf", "bfloat16", "Z0 Z1 Y0 Y1", 2048)
 _decl("sbuf", "bfloat16", "XL", 768)
 _decl("sbuf", "bfloat16", "yy y0 y01", 256)
@@ -29,23 +31,23 @@ _decl("sbuf", "float32", "SA0 SA1 KX RS pm", 128)
 _decl("sbuf", "float32", "onef D160", 160)
 _decl("sbuf", "float16", "Ev Od", 160)
 _decl("sbuf", "float16", "I16", 128)
-_decl("sbuf", "bfloat16", "IB NI oneb MK SX", 128)
+_decl("sbuf", "bfloat16", "IB NI oneb MK", 128)
 _decl("sbuf", "float32", "W", 8)
-_decl("sbuf", "bfloat16", "W1 W2 Wb SW", 8)
-_decl("sbuf", "int32", "e15 e1", 8)
-_decl("sbuf", "uint16", "e15u e1u", 8)
-_decl("sbuf", "float16", "base", 16)
+_decl("sbuf", "bfloat16", "W1 W2", 8)
+_decl("sbuf", "bfloat16", "SW", 144)
+_decl("sbuf", "int32", "e15", 8)
+_decl("sbuf", "uint16", "e15u", 8)
 _decl("sbuf", "int32", "lci upi", 48)
 _decl("sbuf", "int32", "thi", 3, 8)
 _decl("sbuf", "float32", "thf", 3, 8)
 _decl("sbuf", "float32", "tsel", 128, 8)
-_decl("sbuf", "int32", "wti ai ai2 pi pg p15", 1)
-_decl("sbuf", "float32", "wtf cnt af par npar p8 p15f c4k", 1)
+_decl("sbuf", "int32", "wti pi pg p15", 1)
+_decl("sbuf", "float32", "wtf cnt a1 af par npar p8 p15f c4k", 1)
 _decl("sbuf", "float32", "thk Tk", 3)
-_decl("sbuf", "int32", "exi b128 z32 nn t1 bi si sm rz0", 16)
+_decl("sbuf", "int32", "exi b128 base z32 nn t1 bi si sm sa rz0", 16)
 _decl("sbuf", "uint16", "Eu nu bu wu", 16)
-_decl("sbuf", "float32", "mone Ep nEp u1 w1 u2 w2 n2 a2 nE sB g1 Tg1 Tg2 g2 px pa", 16)
-_decl("sbuf", "float32", "s2 dd sd P Pu rz K32", 32)
+_decl("sbuf", "float32", "mone Ep nEp u1 w1 u2 w2 n2 a2 nE sB g1 Tg1 Tg2 g2 px pa za s1", 16)
+_decl("sbuf", "float32", "s2 dd sd P Pu rz K32 LS LW", 32)
 _decl("sbuf", "int32", "rk", 32)
 _decl("sbuf", "uint16", "Lu yu", 48)
 _decl("sbuf", "float32", "LA cdum", 48)
@@ -57,11 +59,11 @@ _decl("sbuf", "float32", "land", 5 * 80)
 _decl("sbuf", "float32", "src", 4 * 80)
 
 SEMAPHORES = ["cv", "cs", "cp", "cg", "ls", "dfa", "dfw", "dx", "dy0", "dy1", "dlc", "dup", "dex", "dth", "dwt"]
-SEMAPHORES += ["do%d" % i for i in range(6)]
-SEMAPHORES += ["ar%d%s" % (t, k) for t in range(1, 5) for k in "ABC"]
+SEMAPHORES += ["do%d" % i for i in range(5)]
+SEMAPHORES += ["ar%d%s" % (t, k) for t in range(1, 5) for k in "AB"]
 
 CYC, PEC, GATHER, SCATTER, HOP, CROSS, FAR = 0.00088, 0.00060, 1.56, 3.8, 0.12, 0.27, 5.0
-AHEAD, ROUNDS = 40.0, 4
+AHEAD, ROUNDS, LOADS = 40.0, 2500, 5
 ORDER = []
 
 
@@ -89,39 +91,56 @@ def issue_order(jobs):
         if jobs[i][6] and succ[i]:
             place[i] = min(place[j] for j in succ[i]) - AHEAD * (jobs[i][4] + jobs[i][5] + HOP)
 
+    busy = [j[4] for j in jobs]
+
     def gap(i, j):
         return jobs[i][5] + (CROSS if jobs[i][0] != jobs[j][0] else 0.0 if jobs[i][0] == "p" else HOP)
+    ahead = [[(j, busy[j] + gap(j, i)) for j in pred[i]] for i in range(n)]
+    behind = [[(j, busy[j] + gap(i, j)) for j in succ[i]] for i in range(n)]
 
-    def lay(key, before_, after_, back):
-        at, taken, left = [0.0] * n, {}, [len(p) for p in before_]
-        ready = sorted((key[i], i) for i in range(n) if not left[i])
+    def lay(key, back=False):
+        waits, frees = (behind, pred) if back else (ahead, succ)
+        at, taken, left = [0.0] * n, {}, [len(p) for p in waits]
+        ready = [(key[i], i) for i in range(n) if not left[i]]
         while ready:
-            i = ready.pop(0)[1]
-            t = max([at[j] + jobs[j][4] + (gap(i, j) if back else gap(j, i)) for j in before_[i]] + [jobs[i][5] if back else 0.0])
+            first = min(ready)
+            ready.remove(first)
+            i = first[1]
+            t = jobs[i][5] if back else 0.0
+            for j, d in waits[i]:
+                t = max(t, at[j] + d)
             line = taken.setdefault(jobs[i][0], [])
             k = len(line)
             while k and line[k - 1][1] > t:
                 k -= 1
-            while k < len(line) and line[k][0] < t + jobs[i][4]:
+            while k < len(line) and line[k][0] < t + busy[i] - 1e-9:
                 t = max(t, line[k][1])
                 k += 1
-            line.insert(k, (t, t + jobs[i][4]))
+            line.insert(k, (t, t + busy[i]))
             at[i] = t
-            for j in after_[i]:
+            for j in frees[i]:
                 left[j] -= 1
                 if not left[j]:
                     ready.append((key[j], j))
-            ready.sort()
         return at
-    best, key = None, place
+
+    def settle(key):
+        at = lay(key)
+        late = lay([-at[i] - busy[i] for i in range(n)], True)
+        at = lay([-late[i] - busy[i] for i in range(n)])
+        return max(at[i] + busy[i] + jobs[i][5] for i in range(n)), at
+    seed = [1]
+
+    def draw():
+        seed[0] = seed[0] * 48271 % 2147483647
+        return seed[0] / 2147483647.0
+    best = settle(place)
     for _ in range(ROUNDS):
-        at = lay(key, pred, succ, False)
-        end = max(at[i] + jobs[i][4] + jobs[i][5] for i in range(n))
-        if best is None or end < best[0]:
-            best = (end, at)
-        late = lay([-at[i] - jobs[i][4] for i in range(n)], succ, pred, True)
-        key = [-late[i] - jobs[i][4] for i in range(n)]
-    return sorted(range(n), key=lambda i: (best[1][i], i))
+        mid, wide, shake = draw() * best[0], 2 + 8 * draw(), 1.2 * draw()
+        trial = settle([t + (shake * (draw() - 0.5) if abs(t - mid) < wide else 0.0) for t in best[1]])
+        if trial[0] <= best[0]:
+            best = trial
+    return sorted(range(n), key=lambda i: (i >= LOADS, best[1][i] if i >= LOADS else 0.0, i))
 
 
 def rank_program(g, core, T, topo):
@@ -178,6 +197,8 @@ def rank_program(g, core, T, topo):
             count[q] += 1
             ins.then_inc(T.sem["c" + q], 1)
             after(q, "c" + q, count[q], r, w)
+        if q in "vs" and any(x in SCRATCH and SCRATCH[x][0] == "psum" for x in w):
+            busy += 0.02
         jobs.append((q, issue, r, w, busy, 0.0, lazy[0]))
 
     def dma(q, out, in_, sem, total, r, w, late=2.0):
@@ -190,7 +211,7 @@ def rank_program(g, core, T, topo):
         jobs.append((q, issue, r, w, 0.06, late, lazy[0]))
 
     def cyc(n):
-        return max(n, 64) * CYC
+        return 0.035 + max(n, 50) * CYC
 
     def gat(n):
         return 0.06 + n * GATHER * CYC
@@ -211,7 +232,7 @@ def rank_program(g, core, T, topo):
         op("v", lambda e: e.memset(o, v), "", w, c)
 
     def act(o, a, f, r, w, c=cyc(0), bias=0.0, scale=1.0):
-        op("s", lambda e: e.activation(out=o, in_=a, func=f, bias=bias, scale=scale), r, w, c)
+        op("s", lambda e: e.activation(out=o, in_=a, func=f, bias=bias, scale=scale), r, w, c + 0.02)
 
     def mms(lst, r, w, n=64):
         def fn(e):
@@ -260,7 +281,6 @@ def rank_program(g, core, T, topo):
     aff(T.W[:], T.W[:], [[16, 8]], OP.is_ge, 15, -1, "W", "W", 8)
     iota(T.pm[:], [[0, 8], [1, 16]], 0, 0, "pm", 128, True)
     iota(T.e15[:], [[16, 8]], 15, 0, "e15", 8)
-    iota(T.e1[:], [[1, 8]], 0, 0, "e1", 8)
     iota(T.b128[:], [[-PAD, 2], [128, 8]], PAD, 0, "b128", 16)
     iota(T.K32[:], [[32, 2], [0, 16]], 32, 0, "K32", 32, True)
     aff(T.tsel[:], T.onef[0:8, 0:128], [[1, 128]], OP.is_ge, 0, -16, "onef", "tsel", 128)
@@ -280,7 +300,7 @@ def rank_program(g, core, T, topo):
     ts(T.Od[:], T.D160[:], T.par[:], None, OP.mult, None, "D160 par", "Od", cyc(160))
     act(T.IB[:], T.D160[:, 16:144], ACT.Copy, "D160", "IB", cyc(128))
     act(T.NI[:], T.D160[:, 16:144], ACT.Copy, "D160", "NI", cyc(128), scale=-1.0)
-    for nm, f in (("W1", 65536.0), ("W2", -131072.0), ("Wb", 1.0)):
+    for nm, f in (("W1", 65536.0), ("W2", -131072.0)):
         act(T[nm][:], T.W[:], ACT.Copy, "W", nm, scale=f)
     cp(T.I16[:], T.D160[:, 16:144], "D160", "I16", cyc(128))
     cp(T.p15f[:], T.p15[:], "p15", "p15f")
@@ -288,11 +308,11 @@ def rank_program(g, core, T, topo):
     ts(T.RS[:], T.RS[:], -LOW, None, OP.add, None, "RS", "RS", cyc(128))
     ts(T.pm[:], T.pm[:], T.p15f[:], None, OP.is_equal, None, "pm p15f", "pm", cyc(128))
     cp(T.e15u[:], T.e15[:], "e15", "e15u")
-    cp(T.e1u[:], T.e1[:], "e1", "e1u")
     ts(T.base[:], T.b128[:], T.p8[:], None, OP.add, None, "b128 p8", "base")
     cp(T.thf[:], T.thi[:], "thi", "thf")
     cp(T.wtf[:], T.wti[:], "wti", "wtf")
-    act(T.SW[:], T.W[:], ACT.Copy, "W wtf", "SW", scale=T.wtf[:])
+    fill(T.SW[:], 0.0, "SW")
+    act(T.SW[:, 15:143:16], T.W[:], ACT.Copy, "W wtf", "SW", scale=T.wtf[:])
     mms([(T.MS[:, 0:3], T.tsel[:], T.thf[:], True, True)], "tsel thf", "MS", 256)
     act(T.thk[:], T.MS[:, 0:3], ACT.Copy, "", "MS thk", scale=65536.0)
     act(T.Tk[:], T.thk[:], ACT.Copy, "thk", "Tk")
@@ -302,28 +322,30 @@ def rank_program(g, core, T, topo):
     ts(T.Eu[:], T.exi[:], float(PAD), None, OP.add, None, "exi", "Eu")
     act(T.nEp[:], T.Ep[:], ACT.Copy, "Ep", "nEp", scale=-1.0)
     cp(T.land[:, 0:16], T.lci[:, 0:16], "lci", "land0A")
-    cp(T.land[:, 32:64], T.lci[:, 16:48], "lci", "land0B land0C")
+    cp(T.land[:, 32:64], T.lci[:, 16:48], "lci", "land0B")
     cp(T.land[:, 16:32], T.upi[:, 16:32], "upi", "land0B")
-    cp(T.land[:, 64:80], T.upi[:, 32:48], "upi", "land0C")
+    cp(T.land[:, 64:80], T.upi[:, 32:48], "upi", "land0B")
 
     MAT = {(0, 0): T.Ev[:, 16:144], (0, 1): T.Ev[:, 0:128], (1, 1): T.Od[:, 16:144], (1, 0): T.Od[:, 32:160]}
     REM = [(77 * t) % 8 for t in range(NV)]
-    MSG = {"A": (0, 16), "B": (16, 48), "C": (48, 80)}
+    MSG = {"A": (0, 16), "B": (16, 80)}
 
     def land(t, a, b):
         return T.land[:, 80 * t + a:80 * t + b]
 
-    def arrive(t, k):
-        a = (0, 32, 48)[k]
-        codes, tok = land(t, a, a + 16), "land%d%s" % (t, "ABC"[k])
-        act(col("LA", k), codes, ACT.Copy, tok, "LA%d" % k, bias=1184.0)
-        ts(col("Lu", k), codes, float(PAD), None, OP.add, None, tok, "Lu%d" % k)
+    def arrive(t, m):
+        a, b, codes, rows = (0, 16, land(t, 0, 16), "0") if m == "A" else (16, 48, land(t, 32, 64), "12")
+        tok = "land%d%s" % (t, m)
+        act(T.LA[:, a:b], codes, ACT.Copy, tok, " ".join("LA" + k for k in rows), bias=1184.0)
+        ts(T.Lu[:, a:b], codes, float(PAD), None, OP.add, None, tok, " ".join("Lu" + k for k in rows))
 
     def masks(t):
         I1, I2, tok = land(t, 16, 32), land(t, 64, 80), "land%dB" % t
         act(T.u1[:], I1, ACT.Relu, tok + " c4k", "u1", scale=4096.0, bias=T.c4k[:])
         tt(T.w1[:], I1, T.nEp[:], OP.mult, tok + " nEp", "w1")
-        tok = "land%dC" % t
+        act(T.s1[:], I1, ACT.Copy, tok, "s1", bias=1.0)
+        tt(col("LS", 0), col("LA", 1), T.s1[:], OP.mult, "LA1 s1", "LS1")
+        tt(col("LW", 0), col("LA", 1), T.w1[:], OP.mult, "LA1 w1", "LW1")
         act(T.u2[:], I2, ACT.Relu, tok, "u2", scale=4096.0)
         act(T.s2[:, 16:32], I2, ACT.Relu, tok, "s21")
         act(T.n2[:], I2, ACT.Relu, tok, "n2", scale=-1.0)
@@ -334,16 +356,23 @@ def rank_program(g, core, T, topo):
     def facts(t, k, h, b, btok):
         a, e = (0, 16) if h is None else (8 * h, 8 * h + 8)
         n, w0 = e - a, 77 * t - REM[t]
-        tt(T.z32[:, a:e], col("LA", k, h), b, OP.mult, toks(btok + " LA%d" % k, h), toks("z32%", h))
+        if k == 0:
+            tt(T.z32[:, a:e], col("LA", 0, h), b, OP.mult, toks(btok + " LA0", h), toks("z32%", h))
+        else:
+            tt(T.za[:, a:e], col("LS", k - 1, h), b, OP.mult, toks(btok + " LS%d" % k, h), toks("za%", h))
+            tt(T.z32[:, a:e], T.za[:, a:e], col("LW", k - 1, h), OP.add, toks("za% LW" + str(k), h), toks("z32%", h))
         ts(T.nn[:, a:e], T.z32[:, a:e], 5, 1023, OP.arith_shift_right, OP.bitwise_and, toks("z32%", h), toks("nn%", h))
         ts(T.nu[:, a:e], T.nn[:, a:e], float(REM[t]), None, OP.add, None, toks("nn%", h), toks("nu%", h))
         cp(T.C[:, 16 * a:16 * e], T.FA[:, w0:FW].indirect(T.nu[:, a:e]), toks("nu% FAx FA1 FA2", h), toks("C%", h), gat(16 * n))
-        op("v", lambda v: v.transpose(out=T.CT[:, 16 * a:16 * e], in_=T.C[:, 16 * a:16 * e]), toks("C%", h), toks("CT%", h), cyc(8 * n))
+        for j in range(a // 2, e // 2):
+            u = j // 4
+            op("v", lambda v, u=u, j=j: v.transpose(out=T.CT[:, 128 * u + j % 4:128 * u + 128:4], in_=T.C[:, 32 * j:32 * j + 32]),
+               "C%d" % u, "CT%d_%d" % (u, j % 4), cyc(24))
 
     def lists(h):
         mms([(T.PB[:, 0:128], T.oneb[32:33, :], T.MK[32:33, 0:128], True, False)], "oneb MK", "PB", 128)
-        mms([(T.PB[:, c:128:8], MAT[(c % 2, x)], T.CT[:, 128 * h + 32 * (c // 2) + 16 * x:128 * h + 32 * (c // 2) + 16 * x + 16],
-              False, c == 7 and x == 1) for c in range(8) for x in range(2)], "CT%d Ev Od" % h, "PB")
+        mms([(T.PB[:, y:128:2], MAT[(y, x)], T.CT[:, 128 * h + 64 * x:128 * h + 64 * x + 64], False, x + y == 2)
+             for y in range(2) for x in range(2)], " ".join("CT%d_%d" % (h, j) for j in range(4)) + " Ev Od", "PB")
         cp(T.CTu[:, 128 * h:128 * h + 128], T.PB[:, 0:128], "", "PB CTu%d" % h, cyc(128))
         KB = T["KB%d" % h][:, 0:128]
         mms([(KB, T.oneb[0:65, :], T.MK[0:65, 0:128], True, False), (KB, T.C[:, 128 * h:128 * h + 128], T.I16[:], False, False)],
@@ -357,39 +386,32 @@ def rank_program(g, core, T, topo):
         else:
             act(o, i, ACT.Copy, r, toks("XL" + str(k) + "_%", h), gat(16 * (e - a)))
 
-    def qtok(h, n):
-        return " ".join("Q%d_%d" % (h, i) for i in (1, 2, 4) if i < 2 * n)
-
     def qpart(k, h, off, otok):
         Q = T["Q%d" % h]
         tt(Q[:, 0:128], Xw.indirect(off), T.XL[:, 256 * k + 128 * h:256 * k + 128 * h + 128], OP.max,
-           "%s %s XL%d_%d" % (XT, otok, k, h), "Q%d_1" % h, gat(128))
-        for n in (1, 2):
-            cp(Q[:, 128 * n:256 * n], Q[:, 0:128 * n], qtok(h, n), "Q%d_%d" % (h, 2 * n), cyc(64 * n))
+           "%s %s XL%d_%d" % (XT, otok, k, h), "Q%d_0" % h, gat(128))
+        for n in range(1, max(e - a for (who, a, e) in CHUNKS[k][h] if who == "A")):
+            cp(Q[:, 128 * n:128 * n + 128], Q[:, 0:128], "Q%d_0" % h, "Q%d_%d" % (h, n), cyc(64))
 
     bank = [0]
 
-    def main(h):
+    def main(k, h):
         Z, Y, Q, kb = T["Z%d" % h], T["Y%d" % h], T["Q%d" % h], "KB%d" % h
-        for (who, a, e) in CHUNKS:
-            n, z, tok = e - a, Z[:, 128 * a:128 * e], "Z%d_%d" % (h, a)
-            lst, sums = Xw.indirect(T.CTu[:, 128 * h + 8 * a:128 * h + 8 * e]), [(Z, T.W1)]
-            if who != "D":
-                tt(z, lst, Q[:, 0:128 * n], OP.subtract, "%s CTu%d %s" % (XT, h, qtok(h, n)), tok, gat(128 * n))
+        for (who, a, e) in CHUNKS[k][h]:
+            n, z, tok = e - a, Z[:, 128 * a:128 * e], " ".join("Z%d_%d" % (h, m) for m in range(a, e))
+            lst = Xw.indirect(T.CTu[:, 128 * h + 8 * a:128 * h + 8 * e])
             if who == "A":
-                sums, src = [(Y, T.W2), (Z, T.W1)], tok
-                for u in range(a, e, 2):
-                    v = min(u + 2, e)
-                    tok += " Y%d_%d" % (h, u)
-                    ts(Y[:, 128 * u:128 * v], Z[:, 128 * u:128 * v], 0.0, None, OP.min, None, src, "Y%d_%d" % (h, u), cyc(64 * (v - u)))
-            elif who == "B":
-                act(z, z, ACT.Abs, tok, tok, cyc(128 * n))
+                sums, cut = [(Y, T.W2), (Z, T.W1)], tok.replace("Z", "Y")
+                tt(z, lst, Q[:, 0:128 * n], OP.subtract,
+                   "%s CTu%d %s" % (XT, h, " ".join("Q%d_%d" % (h, u) for u in range(n))), tok, gat(128 * n))
+                ts(Y[:, 128 * a:128 * e], z, 0.0, None, OP.min, None, tok, cut, cyc(70 * n))
+                tok += " " + cut
             else:
-                d = "D%d" % bank[0]
+                sums, d = [(Z, T.W1)], "D%d" % bank[0]
                 bank[0] = (bank[0] + 1) % 3
                 act(z, lst, ACT.Copy, "%s CTu%d" % (XT, h), tok, gat(128 * n))
-                mms([(T[d][:, 0:128 * n], T.NI[:], Q[:, 0:128 * n], True, False)], "NI " + qtok(h, n), d, 128 * n)
-                mms([(T[d][:, 0:128 * n], T.IB[:], z, False, True)], "IB " + tok, d, 128 * n)
+                mms([(T[d][:, 0:128 * n], T.IB[:], z, True, False)], "IB " + tok, d, 128 * n)
+                mms([(T[d][:, 128 * u:128 * u + 128], T.NI[:], Q[:, 0:128], False, u == n - 1) for u in range(n)], "NI Q%d_0" % h, d, 128)
                 act(z, T[d][:, 0:128 * n], ACT.Abs, "", d + " " + tok, cyc(128 * n))
             mms([(T[kb][:, m:128:16], src[:, 128 * m:128 * m + 128], w[:], False, m == 15 and src is Z)
                  for m in range(a, e) for (src, w) in sums], tok + " W1 W2", kb)
@@ -410,7 +432,7 @@ def rank_program(g, core, T, topo):
         least(k - 1, h)
         tt(col("t1", 0, h), col("B", k - 1, h), col("u%d" % k, 0, h), OP.min, "B%d_%d u%d" % (k - 1, h, k), "t1%d" % h)
         tt(col("bi", 0, h), col("t1", 0, h), col("w%d" % k, 0, h), OP.max, "t1%d w%d" % (h, k), "bi%d" % h)
-        facts(t, k, h, col("bi", 0, h), "bi%")
+        facts(t, k, h, col("B", k - 1, h), "B%d_%%" % (k - 1))
         cp(col("bu", 0, h), col("bi", 0, h), "bi%d" % h, "bu%d" % h)
         qpart(k, h, col("bu", 0, h), "bu%d" % h)
         lists(h)
@@ -442,6 +464,8 @@ def rank_program(g, core, T, topo):
         act(T.Tg1[:], T.g1[:], ACT.Copy, "g1 Tk", "Tg1", scale=T.Tk[:, 1:2], bias=-LOW)
         tt(T.sB[:], T.s2[:, 0:16], col("B", 0), OP.mult, "s20 B0_0 B0_1", "sB")
         tt(T.w2[:], T.sB[:], T.nE[:], OP.add, "sB nE", "w2")
+        tt(col("LS", 1), col("LA", 2), T.s2[:, 16:32], OP.mult, "LA2 s21", "LS2")
+        tt(col("LW", 1), col("LA", 2), T.w2[:], OP.mult, "LA2 w2", "LW2")
         tt(T.rz0[:], col("LA", 0), T.exi[:], OP.mult, "LA0 exi", "rz0")
         ts(T.NW[:, 0:16], T.rz0[:], 5, 2047, OP.arith_shift_right, OP.bitwise_and, "rz0", "NW0")
         tt(T.df[:, 0:16], T.NW[:, 0:16], land(t, 0, 16), OP.subtract, "NW0 land%dA" % t, "dfA")
@@ -468,9 +492,8 @@ def rank_program(g, core, T, topo):
         ts(T.NW[:, 16:32], lvc(0), -1.0, None, OP.add, None, "lv0", "NW1")
         act(T.pa[:], lvc(1), ACT.Copy, "lv1", "pa", scale=2.0, bias=-1.0)
         tt(T.NW[:, 64:80], T.NW[:, 16:32], T.pa[:], OP.max, "NW1 pa", "NW2")
-        tt(T.df[:, 16:80], T.NW[:, 16:80], land(t, 16, 80), OP.subtract, "NWl NW1 NW2 land%dB land%dC" % (t, t), "dfB", cyc(128))
+        tt(T.df[:, 16:80], T.NW[:, 16:80], land(t, 16, 80), OP.subtract, "NWl NW1 NW2 land%dB" % t, "dfB", cyc(128))
         act(T.lv[:, 32:48], lvc(1), ACT.Copy, "lv1", "lv1d")
-        send(t, "B", "lv1 lv1d")
 
     def write(t, h):
         s = slice(8 * h, 8 * h + 8)
@@ -478,13 +501,12 @@ def rank_program(g, core, T, topo):
         cp(col("yu", 2, h), col("B", 2, h), "B2_%d" % h, "yu2_%d" % h)
         y = T.yy[:, 128 * h:128 * h + 128]
         tt(y, Xw.indirect(col("yu", 2, h)), T.y01[:, 128 * h:128 * h + 128], OP.max, XT + " yu2_%d y01%d" % (h, h), "yy%d" % h, gat(128))
-        mms([(T.MS[:, 0:8], y, T.SW[:], True, True)], "SW yy%d" % h, "MS")
+        mms([(T.MS[:, 0:8], T.SW[:, 15 - p:143 - p], T.yy[:, 128 * h + p:128 * h + 128:16], p == 0, p == 15) for p in range(16)],
+            "SW yy%d" % h, "MS")
         cp(T.si[:, s], T.MS[:, 0:8], "", "MS si%d" % h)
         ts(T.sm[:, s], T.si[:, s], 7, None, OP.bitwise_and, None, "si%d" % h, "sm%d" % h)
-        tt(T.SX[:], T.sm[:, s].indirect(T.e1u[:, 0:8]), T.pm[:], OP.mult, "sm%d e1u pm" % h, "SX", gat(128))
-        mms([(T.MS[:, 0:8], T.I16[:], T.base[:, s], True, False)], "I16 base", "MS")
-        mms([(T.MS[:, 0:8], T.SX[:], T.Wb[:], False, True)], "SX Wb", "MS")
-        cp(T.wu[:, s], T.MS[:, 0:8], "", "MS wu%d" % h)
+        tt(T.sa[:, s], T.sm[:, s], T.base[:, s], OP.add, "sm%d base" % h, "sa%d" % h)
+        cp(T.wu[:, s], T.sa[:, s], "sa%d" % h, "wu%d" % h)
 
     def scatter(t, h):
         M = PAD + 1024
@@ -499,9 +521,11 @@ def rank_program(g, core, T, topo):
             "oneb lv0 lv1 lv2_48", "MS")
         op("s", lambda e: e.activation(out=T.cdum[:], in_=T.MS[:, 0:48], func=ACT.Copy, bias=128.0, scale=-1.0,
                                        accum_out=T.cnt[:]), "", "MS cdum cnt", cyc(90))
-        cp(T.ai[:], T.cnt[:], "cnt", "ai")
-        ts(T.ai2[:], T.ai[:], 31, None, OP.bitwise_and, None, "ai", "ai2")
-        ts(T.af[:], T.ai2[:], 65536.0, None, OP.mult, None, "ai2", "af")
+        M = 1.5 * 2 ** 23
+        act(T.a1[:], T.cnt[:], ACT.Copy, "cnt", "a1", scale=1.0 / 32, bias=-31.0 / 64)
+        act(T.a1[:], T.a1[:], ACT.Copy, "a1", "a1", bias=M)
+        act(T.a1[:], T.a1[:], ACT.Copy, "a1", "a1", scale=-2.0 ** 21, bias=M * 2 ** 21)
+        act(T.af[:], T.cnt[:], ACT.Identity, "cnt a1", "af", scale=65536.0, bias=T.a1[:])
         act(T.Tk[:], T.thk[:], ACT.Identity, "thk af", "Tk", bias=T.af[:])
 
     def aside(*calls):
@@ -510,7 +534,7 @@ def rank_program(g, core, T, topo):
             c[0](*c[1:])
         lazy[0] = False
 
-    arrive(0, 0)
+    arrive(0, "A")
     facts(0, 0, None, T.Ep[:], "Ep")
     dma("y", T.FA[:, 1024:FW], T.FA[:, 0:FW - 1024], "dfw", 16, "FA1 FA2", "FAx")
     lazy[0] = False
@@ -520,42 +544,44 @@ def rank_program(g, core, T, topo):
             lists(h)
             xl(0, h)
             qpart(0, h, col("Eu", 0, h), "Eu")
-        aside((arrive, t, 1), (arrive, t, 2), (masks, t), (xl, 1), (xl, 2))
-        main(0)
-        main(1)
+        aside((arrive, t, "B"), (masks, t), (xl, 1), (xl, 2))
+        main(0, 0)
+        main(0, 1)
         follow(t, 1, 0)
-        main(0)
+        main(1, 0)
         follow(t, 1, 1)
         aside((after0, t))
-        main(1)
+        main(1, 1)
         follow(t, 2, 0)
-        main(0)
+        main(2, 0)
         follow(t, 2, 1)
         aside((after1, t))
         if more:
-            aside((arrive, t + 1, 0), (facts, t + 1, 0, None, T.Ep[:], "Ep"))
-        main(1)
+            aside((arrive, t + 1, "A"), (facts, t + 1, 0, None, T.Ep[:], "Ep"))
+        main(2, 1)
         write(t, 0)
         write(t, 1)
         scatter(t, 0)
         scatter(t, 1)
-        for a in (48, 64):
-            ts(T.lv[:, a:a + 16], col("B", 2), 0.0, None, OP.is_gt, None, "B2_0 B2_1", "lv2_%d" % a)
-        send(t, "C", "lv2_48 lv2_64")
+        ts(lvc(2), col("B", 2), 0.0, None, OP.is_gt, None, "B2_0 B2_1", "lv2_48")
+        if more:
+            act(T.lv[:, 64:80], lvc(2), ACT.Copy, "lv2_48", "lv2_64")
+        else:
+            ts(T.lv[:, 64:80], col("B", 2), 0.0, None, OP.is_gt, None, "B2_0 B2_1", "lv2_64")
+        send(t, "B", "lv1 lv1d lv2_48 lv2_64")
         if more:
             aside((thresholds,))
 
     dma("y", T.yl[:, 0:16], land(NV, 0, 16), "do1", 16, "land%dA" % NV, "out1")
-    dma("y", T.yl[:, 16:32], land(NV, 32, 48), "do2", 16, "land%dB" % NV, "out2")
-    dma("y", T.yi[:, 16:32], land(NV, 16, 32), "do3", 16, "land%dB" % NV, "out3")
-    dma("y", T.yl[:, 32:48], land(NV, 48, 64), "do4", 16, "land%dC" % NV, "out4")
-    dma("s", T.yi[:, 32:48], land(NV, 64, 80), "do5", 16, "land%dC" % NV, "out5")
+    dma("y", T.yl[:, 16:48], land(NV, 32, 64), "do2", 16, "land%dB" % NV, "out2")
+    dma("s", T.yi[:, 16:32], land(NV, 16, 32), "do3", 16, "land%dB" % NV, "out3")
+    dma("y", T.yi[:, 32:48], land(NV, 64, 80), "do4", 16, "land%dB" % NV, "out4")
 
     if not ORDER:
         ORDER.extend(issue_order(jobs))
     for i in ORDER:
         jobs[i][1]()
-    for sem in ["do%d" % i for i in range(6)] + ["dy0", "dy1"]:
+    for sem in ["do%d" % i for i in range(5)] + ["dy0", "dy1"]:
         need("g", sem, 16)
     need("g", "ls", sent[0])
     for q in ("v", "s", "p", "g"):

from concourse.mybir import dt, AluOpType, AxisListType, ActivationFunctionType

OP = AluOpType
ACT = ActivationFunctionType
NV, NR, PAD, FW = 4, 3, 32, 1264
ROT = 864
SIX = [("A", 0, 3), ("D", 3, 7), ("D", 7, 10), ("D", 10, 13), ("A", 13, 16)]
FIVE = [("A", 0, 2), ("D", 2, 6), ("D", 6, 10), ("D", 10, 13), ("A", 13, 16)]
CHUNKS = [[SIX, SIX], [FIVE, FIVE], [FIVE, SIX]]
BIG = 2.0 ** 25
LOW = 240 * 65536.0

SCRATCH = {}


def _decl(where, dtype, names, n, rows=128):
    for nm in names.split():
        SCRATCH[nm] = (where, [rows, n], dtype)


_decl("sbuf", "bfloat16", "X", 2080)
_decl("sbuf", "int32", "FA", FW)
_decl("sbuf", "float16", "C CT", 256)
_decl("sbuf", "uint16", "CTu", 256)
_decl("sbuf", "bfloat16", "Q0 Q1", 384)
_decl("sbuf", "bfloat16", "Z0 Z1 Y0 Y1", 2048)
_decl("sbuf", "bfloat16", "XL", 768)
_decl("sbuf", "bfloat16", "yy y0 y01", 256)
_decl("psum", "float32", "KB0 KB1 KN PB MS D0 D1 D2", 512)
_decl("sbuf", "float32", "SA0 SA1 KX RS pm", 128)
_decl("sbuf", "float32", "onef D160", 160)
_decl("sbuf", "float16", "Ev Od", 160)
_decl("sbuf", "float16", "I16", 128)
_decl("sbuf", "bfloat16", "IB NI oneb MK", 128)
_decl("sbuf", "float32", "W", 8)
_decl("sbuf", "bfloat16", "W1 W2", 8)
_decl("sbuf", "bfloat16", "SW", 144)
_decl("sbuf", "int32", "e15", 8)
_decl("sbuf", "uint16", "e15u", 8)
_decl("sbuf", "int32", "lci upi", 48)
_decl("sbuf", "int32", "thi", 3, 8)
_decl("sbuf", "float32", "thf", 3, 8)
_decl("sbuf", "float32", "tsel", 128, 8)
_decl("sbuf", "int32", "wti pi pg p15", 1)
_decl("sbuf", "float32", "wtf cnt a1 af par npar p8 p15f c4k", 1)
_decl("sbuf", "float32", "thk Tk", 3)
_decl("sbuf", "int32", "exi b128 base z32 nn t1 bi si sm sa rz0", 16)
_decl("sbuf", "uint16", "Eu nu bu wu", 16)
_decl("sbuf", "float32", "mone Ep nEp u1 w1 u2 w2 n2 a2 nE sB g1 Tg1 Tg2 g2 px pa za s1", 16)
_decl("sbuf", "float32", "s2 dd sd P Pu rz K32 LS LW", 32)
_decl("sbuf", "int32", "rk", 32)
_decl("sbuf", "uint16", "Lu yu", 48)
_decl("sbuf", "float32", "LA cdum", 48)
_decl("sbuf", "int32", "K B", 48)
_decl("sbuf", "int32", "NW", 80)
_decl("sbuf", "float32", "df xx", 80)
_decl("sbuf", "bfloat16", "lv", 80)
_decl("sbuf", "float32", "land", 5 * 80)
_decl("sbuf", "float32", "src", 4 * 80)

SEMAPHORES = ["cv", "cs", "cp", "cg", "ls", "dfa", "dfw", "dx", "dy0", "dy1", "dlc", "dup", "dex", "dth", "dwt"]
SEMAPHORES += ["do%d" % i for i in range(5)]
SEMAPHORES += ["ar%d%s" % (t, k) for t in range(1, 5) for k in "AB"]

CYC, PEC, GATHER, SCATTER, HOP, CROSS, FAR = 0.00088, 0.00060, 1.56, 3.8, 0.12, 0.27, 5.0
AHEAD, ROUNDS, LOADS = 40.0, 2500, 5
ORDER = []


def issue_order(jobs):
    n = len(jobs)
    pred, succ = [set() for _ in range(n)], [[] for _ in range(n)]
    lastw, readers = {}, {}
    for i, (q, fn, r, w, busy, late, lazy) in enumerate(jobs):
        for b in r:
            if b in lastw:
                pred[i].add(lastw[b])
        for b in w:
            if b in lastw:
                pred[i].add(lastw[b])
            pred[i].update(readers.get(b, ()))
        pred[i].discard(i)
        for b in r:
            readers.setdefault(b, []).append(i)
        for b in w:
            lastw[b], readers[b] = i, []
        for j in pred[i]:
            succ[j].append(i)
    place = list(range(n))
    for i in range(n - 1, -1, -1):
        if jobs[i][6] and succ[i]:
            place[i] = min(place[j] for j in succ[i]) - AHEAD * (jobs[i][4] + jobs[i][5] + HOP)

    busy = [j[4] for j in jobs]

    def gap(i, j):
        return jobs[i][5] + (CROSS if jobs[i][0] != jobs[j][0] else 0.0 if jobs[i][0] == "p" else HOP)
    ahead = [[(j, busy[j] + gap(j, i)) for j in pred[i]] for i in range(n)]
    behind = [[(j, busy[j] + gap(i, j)) for j in succ[i]] for i in range(n)]

    def lay(key, back=False):
        waits, frees = (behind, pred) if back else (ahead, succ)
        at, taken, left = [0.0] * n, {}, [len(p) for p in waits]
        ready = [(key[i], i) for i in range(n) if not left[i]]
        while ready:
            first = min(ready)
            ready.remove(first)
            i = first[1]
            t = jobs[i][5] if back else 0.0
            for j, d in waits[i]:
                t = max(t, at[j] + d)
            line = taken.setdefault(jobs[i][0], [])
            k = len(line)
            while k and line[k - 1][1] > t:
                k -= 1
            while k < len(line) and line[k][0] < t + busy[i] - 1e-9:
                t = max(t, line[k][1])
                k += 1
            line.insert(k, (t, t + busy[i]))
            at[i] = t
            for j in frees[i]:
                left[j] -= 1
                if not left[j]:
                    ready.append((key[j], j))
        return at

    def settle(key):
        at = lay(key)
        late = lay([-at[i] - busy[i] for i in range(n)], True)
        at = lay([-late[i] - busy[i] for i in range(n)])
        return max(at[i] + busy[i] + jobs[i][5] for i in range(n)), at
    seed = [1]

    def draw():
        seed[0] = seed[0] * 48271 % 2147483647
        return seed[0] / 2147483647.0
    best = settle(place)
    for _ in range(ROUNDS):
        mid, wide, shake = draw() * best[0], 2 + 8 * draw(), 1.2 * draw()
        trial = settle([t + (shake * (draw() - 0.5) if abs(t - mid) < wide else 0.0) for t in best[1]])
        if trial[0] <= best[0]:
            best = trial
    return sorted(range(n), key=lambda i: (i >= LOADS, best[1][i] if i >= LOADS else 0.0, i))


def rank_program(g, core, T, topo):
    rank = T.rank_of(core)
    if rank is None:
        return
    n_ranks = len(T.cores)
    QUEUE = {"v": g.vector, "s": g.scalar, "p": g.tensor, "g": g, "y": g.sync}
    count = {"v": 0, "s": 0, "p": 0, "g": 0}
    known = {q: {} for q in QUEUE}
    snap, lastw, readers, sent, jobs, lazy = {}, {}, {}, [0], [], [False]

    def need(q, sem, val):
        if known[q].get(sem, 0) >= val:
            return
        QUEUE[q].wait_ge(T.sem[sem], val)
        for s_, v_ in snap.get((sem, val), {}).items():
            if known[q].get(s_, 0) < v_:
                known[q][s_] = v_
        known[q][sem] = val

    def before(q, r, w):
        deps = {}

        def add(d):
            if deps.get(d[0], 0) < d[1]:
                deps[d[0]] = d[1]
        for b in r:
            if b in lastw:
                add(lastw[b])
        for b in w:
            if b in lastw and not (lastw[b][2] == q and q == "p"):
                add(lastw[b])
            for d in readers.get(b, ()):
                add(d)
        for sem in sorted(deps, key=lambda s_: -len(snap.get((s_, deps[s_]), {}))):
            need(q, sem, deps[sem])

    def after(q, sem, val, r, w):
        d = (sem, val, q)
        for b in r:
            readers.setdefault(b, []).append(d)
        for b in w:
            lastw[b] = d
            readers[b] = []
        snap[(sem, val)] = dict(known[q])

    def op(q, fn, r, w, busy):
        r, w = r.split(), w.split()

        def issue():
            before(q, r, w)
            ins = fn(QUEUE[q])
            count[q] += 1
            ins.then_inc(T.sem["c" + q], 1)
            after(q, "c" + q, count[q], r, w)
        if q in "vs" and any(x in SCRATCH and SCRATCH[x][0] == "psum" for x in w):
            busy += 0.02
        jobs.append((q, issue, r, w, busy, 0.0, lazy[0]))

    def dma(q, out, in_, sem, total, r, w, late=2.0):
        r, w = r.split(), w.split()

        def issue():
            before(q, r, w)
            QUEUE[q].dma_start(out=out, in_=in_).then_inc(T.sem[sem], 16)
            after(q, sem, total, r, w)
        jobs.append((q, issue, r, w, 0.06, late, lazy[0]))

    def cyc(n):
        return 0.035 + max(n, 50) * CYC

    def gat(n):
        return 0.06 + n * GATHER * CYC

    def tt(o, a, b, f, r, w, c=cyc(0)):
        op("v", lambda e: e.tensor_tensor(out=o, in0=a, in1=b, op=f), r, w, c)

    def ts(o, a, s1, s2, f0, f1, r, w, c=cyc(0)):
        if s2 is None:
            op("v", lambda e: e.tensor_scalar(out=o, in0=a, scalar1=s1, scalar2=None, op0=f0), r, w, c)
        else:
            op("v", lambda e: e.tensor_scalar(out=o, in0=a, scalar1=s1, scalar2=s2, op0=f0, op1=f1), r, w, c)

    def cp(o, a, r, w, c=cyc(0)):
        op("v", lambda e: e.tensor_copy(out=o, in_=a), r, w, c)

    def fill(o, v, w, c=cyc(0)):
        op("v", lambda e: e.memset(o, v), "", w, c)

    def act(o, a, f, r, w, c=cyc(0), bias=0.0, scale=1.0):
        op("s", lambda e: e.activation(out=o, in_=a, func=f, bias=bias, scale=scale), r, w, c + 0.02)

    def mms(lst, r, w, n=64):
        def fn(e):
            ins = None
            for (o, a, b, st, sp) in lst:
                ins = e.matmul(out=o, lhsT=a, rhs=b, start=st, stop=sp)
            return ins
        op("p", fn, r, w, len(lst) * max(n, 64) * PEC)

    def aff(o, a, pat, f, base, cm, r, w, n):
        op("g", lambda e: e.affine_select(o, a, pat, f, 0.0, base, cm), r, w, 0.19 + 2 * n * CYC)

    def iota(o, pat, base, cm, w, n, small=False):
        if small:
            op("g", lambda e: e.iota(o, pat, base, cm, allow_small_or_imprecise_dtypes=True), "", w, 0.15 + 2 * n * CYC)
        else:
            op("g", lambda e: e.iota(o, pat, base, cm), "", w, 0.15 + 2 * n * CYC)

    def col(nm, k, h=None):
        a = 16 * k
        return T[nm][:, a:a + 16] if h is None else T[nm][:, a + 8 * h:a + 8 * h + 8]

    def toks(s, h):
        return " ".join(x.replace("%", str(u)) for x in s.split() for u in ((0, 1) if h is None else (h,)))

    Xw, XT = T.X[:, 0:2080], "X0 X1 Xpad"

    dma("y", T.exi[:], T.ex[:], "dex", 16, "", "exi")
    dma("s", T.lci[:], T.lc[:], "dlc", 16, "", "lci")
    dma("y", T.FA[:, 1024 - ROT:1024], T.fa[:, 0:ROT], "dfa", 32, "", "FA1", 3.5)
    dma("s", T.FA[:, 0:1024 - ROT], T.fa[:, ROT:1024], "dfa", 32, "", "FA2", 3.5)
    dma("s", T.X[:, PAD:PAD + 2048], T.xs[:], "dx", 16, "", "X0 X1", 4.5)
    lazy[0] = True
    dma("y", T.upi[:], T.up[:], "dup", 16, "FA1", "upi", 3.0)
    dma("y", T.thi[:], T.th[:], "dth", 16, "FA1", "thi", 3.0)
    dma("y", T.wti[:], T.wt[:], "dwt", 16, "FA1", "wti", 3.0)

    fill(T.onef[:], 1.0, "onef", cyc(160))
    iota(T.pi[:], [[0, 1]], 0, 1, "pi", 1)
    aff(T.D160[:], T.onef[:], [[-1, 160]], OP.is_equal, 16, 1, "onef", "D160", 160)
    fill(T.MK[:], 0.0, "MK")
    iota(T.MK[0:1, :], [[0, 8], [4096, 16]], 0, 0, "MK", 128, True)
    fill(T.MK[32:33, :], float(PAD), "MK")
    fill(T.MK[64:65, :], -LOW, "MK")
    aff(T.W[:], T.onef[:, 0:8], [[-16, 8]], OP.is_ge, 0, 1, "onef", "W", 8)
    aff(T.W[:], T.W[:], [[16, 8]], OP.is_ge, 15, -1, "W", "W", 8)
    iota(T.pm[:], [[0, 8], [1, 16]], 0, 0, "pm", 128, True)
    iota(T.e15[:], [[16, 8]], 15, 0, "e15", 8)
    iota(T.b128[:], [[-PAD, 2], [128, 8]], PAD, 0, "b128", 16)
    iota(T.K32[:], [[32, 2], [0, 16]], 32, 0, "K32", 32, True)
    aff(T.tsel[:], T.onef[0:8, 0:128], [[1, 128]], OP.is_ge, 0, -16, "onef", "tsel", 128)
    aff(T.tsel[:], T.tsel[:], [[-1, 128]], OP.is_ge, 15, 16, "tsel", "tsel", 128)

    fill(T.FA[:, 1024:FW], 0, "FAx", cyc(240))
    fill(T.X[:, 0:PAD], 0.0, "Xpad")
    fill(T.oneb[:], 1.0, "oneb")
    fill(T.mone[:], -1.0, "mone")
    fill(T.c4k[:], 4096.0, "c4k")
    ts(T.pg[:], T.pi[:], 4, 1, OP.arith_shift_right, OP.bitwise_and, "pi", "pg")
    ts(T.p15[:], T.pi[:], 15, None, OP.bitwise_and, None, "pi", "p15")
    cp(T.par[:], T.pg[:], "pg", "par")
    ts(T.npar[:], T.pg[:], -1.0, 1.0, OP.mult, OP.add, "pg", "npar")
    ts(T.p8[:], T.p15[:], 8.0, None, OP.mult, None, "p15", "p8")
    ts(T.Ev[:], T.D160[:], T.npar[:], None, OP.mult, None, "D160 npar", "Ev", cyc(160))
    ts(T.Od[:], T.D160[:], T.par[:], None, OP.mult, None, "D160 par", "Od", cyc(160))
    act(T.IB[:], T.D160[:, 16:144], ACT.Copy, "D160", "IB", cyc(128))
    act(T.NI[:], T.D160[:, 16:144], ACT.Copy, "D160", "NI", cyc(128), scale=-1.0)
    for nm, f in (("W1", 65536.0), ("W2", -131072.0)):
        act(T[nm][:], T.W[:], ACT.Copy, "W", nm, scale=f)
    cp(T.I16[:], T.D160[:, 16:144], "D160", "I16", cyc(128))
    cp(T.p15f[:], T.p15[:], "p15", "p15f")
    ts(T.RS[:], T.pm[:], 0.0, BIG, OP.is_equal, OP.mult, "pm", "RS", cyc(128))
    ts(T.RS[:], T.RS[:], -LOW, None, OP.add, None, "RS", "RS", cyc(128))
    ts(T.pm[:], T.pm[:], T.p15f[:], None, OP.is_equal, None, "pm p15f", "pm", cyc(128))
    cp(T.e15u[:], T.e15[:], "e15", "e15u")
    ts(T.base[:], T.b128[:], T.p8[:], None, OP.add, None, "b128 p8", "base")
    cp(T.thf[:], T.thi[:], "thi", "thf")
    cp(T.wtf[:], T.wti[:], "wti", "wtf")
    fill(T.SW[:], 0.0, "SW")
    act(T.SW[:, 15:143:16], T.W[:], ACT.Copy, "W wtf", "SW", scale=T.wtf[:])
    mms([(T.MS[:, 0:3], T.tsel[:], T.thf[:], True, True)], "tsel thf", "MS", 256)
    act(T.thk[:], T.MS[:, 0:3], ACT.Copy, "", "MS thk", scale=65536.0)
    act(T.Tk[:], T.thk[:], ACT.Copy, "thk", "Tk")
    dma("y", T.yi[:, 0:16], T.mone[:], "do0", 16, "mone", "out0")

    ts(T.Ep[:], T.exi[:], float(PAD), None, OP.add, None, "exi", "Ep")
    ts(T.Eu[:], T.exi[:], float(PAD), None, OP.add, None, "exi", "Eu")
    act(T.nEp[:], T.Ep[:], ACT.Copy, "Ep", "nEp", scale=-1.0)
    cp(T.land[:, 0:16], T.lci[:, 0:16], "lci", "land0A")
    cp(T.land[:, 32:64], T.lci[:, 16:48], "lci", "land0B")
    cp(T.land[:, 16:32], T.upi[:, 16:32], "upi", "land0B")
    cp(T.land[:, 64:80], T.upi[:, 32:48], "upi", "land0B")

    MAT = {(0, 0): T.Ev[:, 16:144], (0, 1): T.Ev[:, 0:128], (1, 1): T.Od[:, 16:144], (1, 0): T.Od[:, 32:160]}
    REM = [(77 * t) % 8 for t in range(NV)]
    MSG = {"A": (0, 16), "B": (16, 80)}

    def land(t, a, b):
        return T.land[:, 80 * t + a:80 * t + b]

    def arrive(t, m):
        a, b, codes, rows = (0, 16, land(t, 0, 16), "0") if m == "A" else (16, 48, land(t, 32, 64), "12")
        tok = "land%d%s" % (t, m)
        act(T.LA[:, a:b], codes, ACT.Copy, tok, " ".join("LA" + k for k in rows), bias=1184.0)
        ts(T.Lu[:, a:b], codes, float(PAD), None, OP.add, None, tok, " ".join("Lu" + k for k in rows))

    def masks(t):
        I1, I2, tok = land(t, 16, 32), land(t, 64, 80), "land%dB" % t
        act(T.u1[:], I1, ACT.Relu, tok + " c4k", "u1", scale=4096.0, bias=T.c4k[:])
        tt(T.w1[:], I1, T.nEp[:], OP.mult, tok + " nEp", "w1")
        act(T.s1[:], I1, ACT.Copy, tok, "s1", bias=1.0)
        tt(col("LS", 0), col("LA", 1), T.s1[:], OP.mult, "LA1 s1", "LS1")
        tt(col("LW", 0), col("LA", 1), T.w1[:], OP.mult, "LA1 w1", "LW1")
        act(T.u2[:], I2, ACT.Relu, tok, "u2", scale=4096.0)
        act(T.s2[:, 16:32], I2, ACT.Relu, tok, "s21")
        act(T.n2[:], I2, ACT.Relu, tok, "n2", scale=-1.0)
        act(T.a2[:], I2, ACT.Abs, tok, "a2")
        act(T.s2[:, 0:16], T.a2[:], ACT.Copy, "a2", "s20", scale=-1.0, bias=1.0)
        tt(T.nE[:], T.n2[:], T.Ep[:], OP.mult, "n2 Ep", "nE")

    def facts(t, k, h, b, btok):
        a, e = (0, 16) if h is None else (8 * h, 8 * h + 8)
        n, w0 = e - a, 77 * t - REM[t]
        if k == 0:
            tt(T.z32[:, a:e], col("LA", 0, h), b, OP.mult, toks(btok + " LA0", h), toks("z32%", h))
        else:
            tt(T.za[:, a:e], col("LS", k - 1, h), b, OP.mult, toks(btok + " LS%d" % k, h), toks("za%", h))
            tt(T.z32[:, a:e], T.za[:, a:e], col("LW", k - 1, h), OP.add, toks("za% LW" + str(k), h), toks("z32%", h))
        ts(T.nn[:, a:e], T.z32[:, a:e], 5, 1023, OP.arith_shift_right, OP.bitwise_and, toks("z32%", h), toks("nn%", h))
        ts(T.nu[:, a:e], T.nn[:, a:e], float(REM[t]), None, OP.add, None, toks("nn%", h), toks("nu%", h))
        cp(T.C[:, 16 * a:16 * e], T.FA[:, w0:FW].indirect(T.nu[:, a:e]), toks("nu% FAx FA1 FA2", h), toks("C%", h), gat(16 * n))
        for j in range(a // 2, e // 2):
            u = j // 4
            op("v", lambda v, u=u, j=j: v.transpose(out=T.CT[:, 128 * u + j % 4:128 * u + 128:4], in_=T.C[:, 32 * j:32 * j + 32]),
               "C%d" % u, "CT%d_%d" % (u, j % 4), cyc(24))

    def lists(h):
        mms([(T.PB[:, 0:128], T.oneb[32:33, :], T.MK[32:33, 0:128], True, False)], "oneb MK", "PB", 128)
        mms([(T.PB[:, y:128:2], MAT[(y, x)], T.CT[:, 128 * h + 64 * x:128 * h + 64 * x + 64], False, x + y == 2)
             for y in range(2) for x in range(2)], " ".join("CT%d_%d" % (h, j) for j in range(4)) + " Ev Od", "PB")
        cp(T.CTu[:, 128 * h:128 * h + 128], T.PB[:, 0:128], "", "PB CTu%d" % h, cyc(128))
        KB = T["KB%d" % h][:, 0:128]
        mms([(KB, T.oneb[0:65, :], T.MK[0:65, 0:128], True, False), (KB, T.C[:, 128 * h:128 * h + 128], T.I16[:], False, False)],
            "oneb MK I16 C%d" % h, "KB%d" % h, 128)

    def xl(k, h=None):
        a, e = (0, 16) if h is None else (8 * h, 8 * h + 8)
        o, i, r = T.XL[:, 256 * k + 16 * a:256 * k + 16 * e], Xw.indirect(col("Lu", k, h)), XT + " Lu%d" % k
        if h == 0:
            cp(o, i, r, "XL%d_0" % k, gat(128))
        else:
            act(o, i, ACT.Copy, r, toks("XL" + str(k) + "_%", h), gat(16 * (e - a)))

    def qpart(k, h, off, otok):
        Q = T["Q%d" % h]
        tt(Q[:, 0:128], Xw.indirect(off), T.XL[:, 256 * k + 128 * h:256 * k + 128 * h + 128], OP.max,
           "%s %s XL%d_%d" % (XT, otok, k, h), "Q%d_0" % h, gat(128))
        for n in range(1, max(e - a for (who, a, e) in CHUNKS[k][h] if who == "A")):
            cp(Q[:, 128 * n:128 * n + 128], Q[:, 0:128], "Q%d_0" % h, "Q%d_%d" % (h, n), cyc(64))

    bank = [0]

    def main(k, h):
        Z, Y, Q, kb = T["Z%d" % h], T["Y%d" % h], T["Q%d" % h], "KB%d" % h
        for (who, a, e) in CHUNKS[k][h]:
            n, z, tok = e - a, Z[:, 128 * a:128 * e], " ".join("Z%d_%d" % (h, m) for m in range(a, e))
            lst = Xw.indirect(T.CTu[:, 128 * h + 8 * a:128 * h + 8 * e])
            if who == "A":
                sums, cut = [(Y, T.W2), (Z, T.W1)], tok.replace("Z", "Y")
                tt(z, lst, Q[:, 0:128 * n], OP.subtract,
                   "%s CTu%d %s" % (XT, h, " ".join("Q%d_%d" % (h, u) for u in range(n))), tok, gat(128 * n))
                ts(Y[:, 128 * a:128 * e], z, 0.0, None, OP.min, None, tok, cut, cyc(70 * n))
                tok += " " + cut
            else:
                sums, d = [(Z, T.W1)], "D%d" % bank[0]
                bank[0] = (bank[0] + 1) % 3
                act(z, lst, ACT.Copy, "%s CTu%d" % (XT, h), tok, gat(128 * n))
                mms([(T[d][:, 0:128 * n], T.IB[:], z, True, False)], "IB " + tok, d, 128 * n)
                mms([(T[d][:, 128 * u:128 * u + 128], T.NI[:], Q[:, 0:128], False, u == n - 1) for u in range(n)], "NI Q%d_0" % h, d, 128)
                act(z, T[d][:, 0:128 * n], ACT.Abs, "", d + " " + tok, cyc(128 * n))
            mms([(T[kb][:, m:128:16], src[:, 128 * m:128 * m + 128], w[:], False, m == 15 and src is Z)
                 for m in range(a, e) for (src, w) in sums], tok + " W1 W2", kb)

    def least(k, h):
        SA = T["SA%d" % h]
        op("v", lambda e: e.tensor_tensor_scan(out=SA[:], data0=T.RS[:], data1=T["KB%d" % h][:, 0:128], initial=BIG,
                                               op0=OP.max, op1=OP.min), "RS", "KB%d SA%d" % (h, h), cyc(128))
        tt(T.KX[:], SA[:, 0:128].indirect(T.e15u[:, 0:8]), T.pm[:], OP.mult, "SA%d e15u pm" % h, "KX", gat(128))
        mms([(T.KN[:, 0:8], T.KX[:], T.W[:], True, True)], "KX W", "KN", 256)
        if k == 0:
            ts(col("K", 0, h), T.KN[:, 0:8], LOW, T.Tk[:, 0:1], OP.add, OP.min, "Tk", "KN K0_%d" % h)
        else:
            tt(col("K", k, h), T.KN[:, 0:8], col("Tg%d" % k, 0, h), OP.min, "Tg%d" % k, "KN K%d_%d" % (k, h))
        ts(col("B", k, h), col("K", k, h), 4095, None, OP.bitwise_and, None, "K%d_%d" % (k, h), "B%d_%d" % (k, h))

    def follow(t, k, h):
        least(k - 1, h)
        tt(col("t1", 0, h), col("B", k - 1, h), col("u%d" % k, 0, h), OP.min, "B%d_%d u%d" % (k - 1, h, k), "t1%d" % h)
        tt(col("bi", 0, h), col("t1", 0, h), col("w%d" % k, 0, h), OP.max, "t1%d w%d" % (h, k), "bi%d" % h)
        facts(t, k, h, col("B", k - 1, h), "B%d_%%" % (k - 1))
        cp(col("bu", 0, h), col("bi", 0, h), "bi%d" % h, "bu%d" % h)
        qpart(k, h, col("bu", 0, h), "bu%d" % h)
        lists(h)

    def lvc(k, h=None):
        return col("lv", (0, 1, 3)[k], h)

    def send(t, m, r):
        a, b = MSG[m]
        tt(T.xx[:, a:b], T.df[:, a:b], T.lv[:, a:b], OP.mult, ("dfA " if m == "A" else "dfB ") + r, "xx" + m, cyc(2 * (b - a)))
        src, tok = T.src[:, 80 * t + a:80 * t + b], "src%d%s" % (t, m)
        tt(src, T.NW[:, a:b], T.xx[:, a:b], OP.subtract, ("NW0" if m == "A" else "NWl NW1 NW2") + " xx" + m, tok, cyc(2 * (b - a)))
        dst = T.cores[(rank + 1) % n_ranks if t < NV - 1 else (rank - t) % n_ranks]
        w = ["land%d%s" % (t + 1, m)]

        def issue():
            before("g", [tok], [])
            rid, pid = topo.addr(dst, core)
            ar = "ar%d%s" % (t + 1, m)
            g.remote_dma(land(t + 1, a, b), src, T.sem[ar], T.sem.ls, pid, rid, topo.mask(core, dst))
            ne = len(topo.engines(core, dst))
            sent[0] += ne
            lastw[w[0]] = (ar, ne, "remote")
        jobs.append(("g", issue, [tok], w, 0.4, FAR if t or m != "A" else FAR + 3.0, lazy[0]))

    def after0(t):
        ts(lvc(0), col("B", 0), 0.0, None, OP.is_gt, None, "B0_0 B0_1", "lv0")
        tt(T.g1[:], lvc(0), land(t, 16, 32), OP.is_gt, "lv0 land%dB" % t, "g1")
        act(T.Tg1[:], T.g1[:], ACT.Copy, "g1 Tk", "Tg1", scale=T.Tk[:, 1:2], bias=-LOW)
        tt(T.sB[:], T.s2[:, 0:16], col("B", 0), OP.mult, "s20 B0_0 B0_1", "sB")
        tt(T.w2[:], T.sB[:], T.nE[:], OP.add, "sB nE", "w2")
        tt(col("LS", 1), col("LA", 2), T.s2[:, 16:32], OP.mult, "LA2 s21", "LS2")
        tt(col("LW", 1), col("LA", 2), T.w2[:], OP.mult, "LA2 w2", "LW2")
        tt(T.rz0[:], col("LA", 0), T.exi[:], OP.mult, "LA0 exi", "rz0")
        ts(T.NW[:, 0:16], T.rz0[:], 5, 2047, OP.arith_shift_right, OP.bitwise_and, "rz0", "NW0")
        tt(T.df[:, 0:16], T.NW[:, 0:16], land(t, 0, 16), OP.subtract, "NW0 land%dA" % t, "dfA")
        send(t, "A", "lv0")

    def after1(t):
        ts(lvc(1), col("B", 1), 0.0, None, OP.is_gt, None, "B1_0 B1_1", "lv1")
        act(T.dd[:], T.lv[:, 0:32], ACT.Copy, "lv0 lv1", "dd", scale=-1.0, bias=1.0)
        tt(T.sd[:], T.s2[:], T.dd[:], OP.mult, "s20 s21 dd", "sd")
        tt(T.g2[:], T.sd[:, 0:16], T.sd[:, 16:32], OP.is_equal, "sd", "g2")
        act(T.Tg2[:], T.g2[:], ACT.Copy, "g2 Tk", "Tg2", scale=T.Tk[:, 2:3], bias=-LOW)
        cp(T.yu[:, 0:32], T.B[:, 0:32], "B0_0 B0_1 B1_0 B1_1", "yu01")
        act(T.y0[:], Xw.indirect(col("yu", 0)), ACT.Copy, XT + " yu01", "y0", gat(256))
        for h in range(2):
            s = slice(128 * h, 128 * h + 128)
            tt(T.y01[:, s], Xw.indirect(col("yu", 1, h)), T.y0[:, s], OP.max, XT + " yu01 y0", "y01%d" % h, gat(128))
        for k in (1, 2):
            tt(T.px[:], col("dd", k - 1), T.Ep[:] if k == 1 else col("P", 0), OP.mult, "dd " + ("Ep", "P1")[k - 1], "px")
            tt(col("P", k - 1), T.px[:], col("B", k - 1), OP.add, "px B%d_0 B%d_1" % (k - 1, k - 1), "P%d" % k)
        act(T.Pu[:], T.P[:], ACT.Copy, "P1 P2", "Pu", bias=-float(PAD))
        tt(T.rz[:], T.LA[:, 16:48], T.Pu[:], OP.mult, "LA1 LA2 Pu", "rz")
        tt(T.rk[:], T.rz[:], T.K32[:], OP.add, "rz K32", "rk")
        ts(T.NW[:, 32:64], T.rk[:], 5, 2047, OP.arith_shift_right, OP.bitwise_and, "rk", "NWl")
        ts(T.NW[:, 16:32], lvc(0), -1.0, None, OP.add, None, "lv0", "NW1")
        act(T.pa[:], lvc(1), ACT.Copy, "lv1", "pa", scale=2.0, bias=-1.0)
        tt(T.NW[:, 64:80], T.NW[:, 16:32], T.pa[:], OP.max, "NW1 pa", "NW2")
        tt(T.df[:, 16:80], T.NW[:, 16:80], land(t, 16, 80), OP.subtract, "NWl NW1 NW2 land%dB" % t, "dfB", cyc(128))
        act(T.lv[:, 32:48], lvc(1), ACT.Copy, "lv1", "lv1d")

    def write(t, h):
        s = slice(8 * h, 8 * h + 8)
        least(2, h)
        cp(col("yu", 2, h), col("B", 2, h), "B2_%d" % h, "yu2_%d" % h)
        y = T.yy[:, 128 * h:128 * h + 128]
        tt(y, Xw.indirect(col("yu", 2, h)), T.y01[:, 128 * h:128 * h + 128], OP.max, XT + " yu2_%d y01%d" % (h, h), "yy%d" % h, gat(128))
        mms([(T.MS[:, 0:8], T.SW[:, 15 - p:143 - p], T.yy[:, 128 * h + p:128 * h + 128:16], p == 0, p == 15) for p in range(16)],
            "SW yy%d" % h, "MS")
        cp(T.si[:, s], T.MS[:, 0:8], "", "MS si%d" % h)
        ts(T.sm[:, s], T.si[:, s], 7, None, OP.bitwise_and, None, "si%d" % h, "sm%d" % h)
        tt(T.sa[:, s], T.sm[:, s], T.base[:, s], OP.add, "sm%d base" % h, "sa%d" % h)
        cp(T.wu[:, s], T.sa[:, s], "sa%d" % h, "wu%d" % h)

    def scatter(t, h):
        M = PAD + 1024
        win = T.X[:, M:M + 1024] if h else T.X[:, 0:M]
        op("v", lambda e: e.tensor_copy(out=win.indirect(T.wu[:, 8 * h:8 * h + 8]), in_=T.yy[:, 128 * h:128 * h + 128]),
           "wu%d yy%d" % (h, h), "X1" if h else "X0 Xpad", 0.06 + 128 * SCATTER * CYC)
        if t == NV - 1:
            dma("sy"[h], T.yx[:, 1024 * h:1024 * h + 1024], T.X[:, PAD + 1024 * h:M + 1024 * h], "dy%d" % h, 16, "X%d" % h, "yx%d" % h, 3.0)

    def thresholds():
        mms([(T.MS[:, 0:32], T.oneb[:], T.lv[:, 0:32], True, True), (T.MS[:, 32:48], T.oneb[:], lvc(2), True, True)],
            "oneb lv0 lv1 lv2_48", "MS")
        op("s", lambda e: e.activation(out=T.cdum[:], in_=T.MS[:, 0:48], func=ACT.Copy, bias=128.0, scale=-1.0,
                                       accum_out=T.cnt[:]), "", "MS cdum cnt", cyc(90))
        M = 1.5 * 2 ** 23
        act(T.a1[:], T.cnt[:], ACT.Copy, "cnt", "a1", scale=1.0 / 32, bias=-31.0 / 64)
        act(T.a1[:], T.a1[:], ACT.Copy, "a1", "a1", bias=M)
        act(T.a1[:], T.a1[:], ACT.Copy, "a1", "a1", scale=-2.0 ** 21, bias=M * 2 ** 21)
        act(T.af[:], T.cnt[:], ACT.Identity, "cnt a1", "af", scale=65536.0, bias=T.a1[:])
        act(T.Tk[:], T.thk[:], ACT.Identity, "thk af", "Tk", bias=T.af[:])

    def aside(*calls):
        lazy[0] = True
        for c in calls:
            c[0](*c[1:])
        lazy[0] = False

    arrive(0, "A")
    facts(0, 0, None, T.Ep[:], "Ep")
    dma("y", T.FA[:, 1024:FW], T.FA[:, 0:FW - 1024], "dfw", 16, "FA1 FA2", "FAx")
    lazy[0] = False
    for t in range(NV):
        more = t < NV - 1
        for h in range(2):
            lists(h)
            xl(0, h)
            qpart(0, h, col("Eu", 0, h), "Eu")
        aside((arrive, t, "B"), (masks, t), (xl, 1), (xl, 2))
        main(0, 0)
        main(0, 1)
        follow(t, 1, 0)
        main(1, 0)
        follow(t, 1, 1)
        aside((after0, t))
        main(1, 1)
        follow(t, 2, 0)
        main(2, 0)
        follow(t, 2, 1)
        aside((after1, t))
        if more:
            aside((arrive, t + 1, "A"), (facts, t + 1, 0, None, T.Ep[:], "Ep"))
        main(2, 1)
        write(t, 0)
        write(t, 1)
        scatter(t, 0)
        scatter(t, 1)
        ts(lvc(2), col("B", 2), 0.0, None, OP.is_gt, None, "B2_0 B2_1", "lv2_48")
        if more:
            act(T.lv[:, 64:80], lvc(2), ACT.Copy, "lv2_48", "lv2_64")
        else:
            ts(T.lv[:, 64:80], col("B", 2), 0.0, None, OP.is_gt, None, "B2_0 B2_1", "lv2_64")
        send(t, "B", "lv1 lv1d lv2_48 lv2_64")
        if more:
            aside((thresholds,))

    dma("y", T.yl[:, 0:16], land(NV, 0, 16), "do1", 16, "land%dA" % NV, "out1")
    dma("y", T.yl[:, 16:48], land(NV, 32, 64), "do2", 16, "land%dB" % NV, "out2")
    dma("s", T.yi[:, 16:32], land(NV, 16, 32), "do3", 16, "land%dB" % NV, "out3")
    dma("y", T.yi[:, 32:48], land(NV, 64, 80), "do4", 16, "land%dB" % NV, "out4")

    if not ORDER:
        ORDER.extend(issue_order(jobs))
    for i in ORDER:
        jobs[i][1]()
    for sem in ["do%d" % i for i in range(5)] + ["dy0", "dy1"]:
        need("g", sem, 16)
    need("g", "ls", sent[0])
    for q in ("v", "s", "p", "g"):
        need("g", "c" + q, count[q])
